import numpy as np
import ml_dtypes


def mxq(x, axis, fmt="e4m3"):
    dtype, down = {"e4m3": (ml_dtypes.float8_e4m3fn, 7), "e5m2": (ml_dtypes.float8_e5m2, 14)}[fmt]
    v = np.moveaxis(np.asarray(x, np.float32).astype(ml_dtypes.bfloat16).astype(np.float64), axis, -1)
    blocks = v.reshape(v.shape[:-1] + (-1, 32))
    amax = np.abs(blocks).max(-1, keepdims=True)
    byte = np.maximum(np.where(amax > 0, np.frexp(amax)[1] - 1 + 127, 0) - down, 1)
    scale = np.exp2(byte - 127.0)
    codes = (blocks / scale).astype(np.float32).astype(dtype).astype(np.float64)
    return np.moveaxis((codes * scale).reshape(v.shape), -1, axis)


WIDE = False


def mx_kscale(k):
    if not WIDE:
        return np.ones(k)
    levels = np.array([24, -24, 12, -12, 0])
    if k % 512:
        return np.exp2(np.random.permutation(np.resize(levels, k // 32))).repeat(32)
    a = np.empty((k // 512, 16))
    for p in range(k // 512):
        a[p, :8] = np.random.permutation(np.resize(levels, 8))
        for g in range(8):
            far = levels[np.abs(levels - a[p, g]) >= 10]
            a[p, g + 8] = far[np.random.randint(len(far))]
    return np.exp2(a.ravel()).repeat(32)


def f64(x):
    return np.asarray(x).astype(np.float64)


def striped(idx):
    return np.tile(idx.reshape(-1, 16).T, (8, 1)).astype(np.uint16)


def unstriped(offs):
    return offs[:16].T.reshape(-1).astype(np.int64)


E2M1 = np.array([0.0, 0.5, 1.0, 1.5, 2.0, 3.0, 4.0, 6.0, -0.0, -0.5, -1.0, -1.5, -2.0, -3.0, -4.0, -6.0])


def pack_weight(w, fmt):
    k, n = w.shape
    w = f64(np.asarray(w, np.float32).astype(ml_dtypes.bfloat16)).reshape(k // 32, 32, n)
    amax = np.abs(w).max(1)
    if fmt == "e4m3":
        byte = np.frexp(amax)[1] - 1 + 127 - 7
    else:
        mant, ex = np.frexp(amax / 6.0)
        byte = np.where(mant > 0.5, ex, ex - 1) + 127
    byte = np.clip(np.where(amax > 0, byte, 1), 1, 254)
    scaled = (w * np.exp2(127.0 - byte)[:, None, :]).reshape(k, n).astype(np.float32)
    by_word = np.ascontiguousarray(scaled.reshape(k // 512, 128, 4, n).transpose(0, 1, 3, 2))
    if fmt == "e4m3":
        words = by_word.astype(ml_dtypes.float8_e4m3fn).view(np.uint8)
    else:
        c = by_word.astype(ml_dtypes.float4_e2m1fn).view(np.uint8) & 0xF
        words = (c[..., 0::2] | (c[..., 1::2] << 4)).reshape(k // 512, 128, 2 * n)
    return np.ascontiguousarray(words), np.ascontiguousarray(byte.astype(np.uint8).reshape(k // 512, 16, n))


def unpack_weight(words, scales, fmt):
    g, _, n = scales.shape
    words = np.ascontiguousarray(words).reshape(g, 128, n, -1)
    if fmt == "e4m3":
        vals = words.view(ml_dtypes.float8_e4m3fn).astype(np.float64)
    else:
        nib = np.empty((g, 128, n, 4), np.uint8)
        nib[..., 0::2] = words & 0xF
        nib[..., 1::2] = words >> 4
        vals = E2M1[nib]
    vals = vals * np.repeat(np.exp2(scales.astype(np.float64) - 127.0), 8, axis=1)[..., None]
    return vals.transpose(0, 1, 3, 2).reshape(g * 512, n)


def pack_table4(v):
    words, scales = pack_weight(v, "e2m1")
    g, t = words.shape[0] // 2, v.shape[1]
    return np.ascontiguousarray(words.reshape(g, 2, 128, t, 2).transpose(0, 2, 3, 1, 4).reshape(g, 128, t, 4)), scales


def unpack_table4(words, scales):
    g, _, t, _ = words.shape
    return unpack_weight(words.reshape(g, 128, t, 2, 2).transpose(0, 3, 1, 2, 4).reshape(2 * g, 128, 2 * t), scales, "e2m1")


K, R, M, N, T, J = 1024, 1024, 512, 512, 4096, 2048


def setup_inputs():
    n = np.random.standard_normal
    s = mx_kscale(K)[:, None]
    s2 = mx_kscale(K)[:, None]
    u = mx_kscale(R)[:, None]
    p_tab = pack_table4(n((K, T)) * s2)
    return {
        "tab_words": p_tab[0],
        "tab_scales": p_tab[1],
        "x": (n((K, M)) * s).astype(np.float32),
        "wq": (n((K, R)) / np.sqrt(K) / s / u.T).astype(np.float32),
        "wk": (n((K, R)) / np.sqrt(K) / s2 * u.T).astype(np.float32),
        "wv": (n((K, N)) / np.sqrt(K) / s2).astype(np.float32),
        "offs": striped(np.random.permutation(T)[:J]),
    }


def reference(tab_words, tab_scales, x, wq, wk, wv, offs):
    idx = unstriped(offs)
    tab_ = unpack_table4(tab_words, tab_scales)[:, idx]
    x_ = mxq(f64(x), 0, "e4m3")
    wq_ = mxq(f64(wq), 0, "e4m3")
    wk_ = mxq(f64(wk), 0, "e4m3")
    qr = wq_.T @ x_
    kr = wk_.T @ tab_
    qa = np.maximum(qr, 0.0)
    ka = np.maximum(kr, 0.0)
    qa_ = mxq(qa, 0, "e4m3")
    ka_ = mxq(ka, 0, "e4m3")
    sc = qa_.T @ ka_
    wv_ = mxq(f64(wv), 0, "e4m3")
    vv = wv_.T @ tab_
    return sc * 0.03125, vv

@@ -1,0 +1,252 @@
+from contextlib import ExitStack
+
+import concourse.mybir as mybir
+
+K, R, M, N, T, J = 1024, 1024, 512, 512, 4096, 2048
+FLOPS = 2 * (K * R * M + K * R * J + R * M * J + K * N * J)
+
+F32 = mybir.dt.float32
+BF16 = mybir.dt.bfloat16
+I32 = mybir.dt.int32
+U32 = mybir.dt.uint32
+U16 = mybir.dt.uint16
+U8 = mybir.dt.uint8
+FP8X4 = mybir.dt.float8_e4m3fn_x4
+FP4X4 = mybir.dt.float4_e2m1fn_x4
+RELU = mybir.ActivationFunctionType.Relu
+COPY = mybir.ActivationFunctionType.Copy
+MAX = mybir.AluOpType.max
+MULT = mybir.AluOpType.mult
+
+P = 128
+PASS = 512
+CHUNK = 512
+SCORE_SCALE = 0.03125
+
+
+def tile_list_kvt_act_kernel(
+    tc, tab_words, tab_scales, x, wq, wk, wv, offs, out_0, out_1
+):
+    nc = tc.nc
+    with ExitStack() as ctx:
+        keep = ctx.enter_context(tc.tile_pool(name="keep", bufs=1))
+        ring = ctx.enter_context(tc.tile_pool(name="ring", bufs=1))
+        psum = ctx.enter_context(tc.psum_pool(name="psum", bufs=8))
+
+        offsets = keep.tile([P, J // 16], U16, name="offsets")
+        table_words = keep.tile([P, T], I32, name="table_words")
+        table_scales = keep.tile([P, T // 4], I32, name="table_scales")
+        picked_scales = keep.tile([P, J], U8, name="picked_scales", align_bytes=64)
+        second_scales = keep.tile([P, J // 4], I32, name="second_scales", align_bytes=64)
+        tab_codes = [keep.tile([P, 2, CHUNK], U16, name="tab_codes%d" % c, align_bytes=64) for c in range(4)]
+
+        def codes_pair(name, width):
+            return (
+                [keep.tile([P, width], U32, name="%s_codes%d" % (name, a), align_bytes=64) for a in range(2)],
+                [keep.tile([P, width], U8, name="%s_scales%d" % (name, a), align_bytes=64) for a in range(2)],
+            )
+
+        wv_c, wv_s = codes_pair("wv", N)
+        wk_c, wk_s = codes_pair("wk", R)
+        wq_c, wq_s = codes_pair("wq", R)
+        x_c, x_s = codes_pair("x", M)
+        qa_c, qa_s = codes_pair("qa", M)
+        ka_c, ka_s = codes_pair("ka", J)
+
+        nc.vector.memset(table_scales[:], 0)
+        nc.vector.memset(second_scales[:], 0)
+        nc.sync.dma_start(offsets[:], offs)
+        nc.sync.dma_start(table_words[:], tab_words[0].rearrange("p t b -> p (t b)").bitcast(I32))
+        rows = tab_scales.bitcast(I32).rearrange("a (q r) t -> r q a t", r=4)
+        for r in range(4):
+            nc.scalar.dma_start(table_scales[r:P:16, :], rows[r])
+
+        def load(w, a, c0, width, tag, bufs):
+            raw = ring.tile([P, 4, width], F32, name=tag, tag=tag, bufs=bufs)
+            nc.sync.dma_start(raw[:], w[PASS * a : PASS * (a + 1), c0 : c0 + width].rearrange("(p j) c -> p j c", j=4))
+            return raw
+
+        wv_raw = {(a, h): load(wv, a, 256 * h, 256, "raw_half", 4) for h in range(2) for a in range(2)}
+        wk_raw = {(a, b): load(wk, a, 512 * b, 512, "raw", 6) for b in range(2) for a in range(2)}
+        x_raw = {a: load(x, a, 0, 512, "raw", 6) for a in range(2)}
+
+        def copy_on(engine, out, in_):
+            if engine == "scalar":
+                nc.scalar.copy(out, in_)
+            else:
+                nc.vector.tensor_copy(out, in_)
+
+        def round_plain(engine, raw, width):
+            grouped = ring.tile([P, 4 * width], BF16, name="grouped", tag="grouped", bufs=4, align_bytes=64)
+            copy_on(
+                engine,
+                grouped[:].rearrange("p (c i j) -> p c j i", i=4, j=4),
+                raw[:].rearrange("p j (c i) -> p c j i", i=4),
+            )
+            return grouped
+
+        def round_permuted(engine, raw):
+            grouped = ring.tile([P, 2048], BF16, name="grouped", tag="grouped", bufs=4, align_bytes=64)
+            copy_on(
+                engine,
+                grouped[:].rearrange("p (t c i j) -> p t c j i", t=4, i=4, j=4),
+                raw[:].rearrange("p j (c t i) -> p t c j i", t=4, i=4),
+            )
+            return grouped
+
+        def quantize(codes, scales, c0, width, grouped):
+            nc.vector.quantize_mx(
+                out=codes[:, c0 : c0 + width].bitcast(FP8X4), scales=scales[:, c0 : c0 + width], in_=grouped
+            )
+
+        def gather_scales(h):
+            cols = slice(1024 * h, 1024 * (h + 1))
+            nc.vector.tensor_copy(
+                picked_scales[:, cols], table_scales[:].bitcast(U8).indirect(offsets[:, 64 * h : 64 * (h + 1)])
+            )
+            words = slice(256 * h, 256 * (h + 1))
+            nc.scalar.dma_start(second_scales[0:112, words], picked_scales[16:P, :].bitcast(I32)[:, words])
+
+        def gather_words(c):
+            picked = ring.tile([P, CHUNK], U32, name="picked", tag="picked", bufs=2)
+            nc.vector.tensor_copy(picked[:], table_words[:].bitcast(U32).indirect(offsets[:, 32 * c : 32 * (c + 1)]))
+            return picked
+
+        def part_words(c, picked):
+            nc.vector.tensor_copy(tab_codes[c][:], picked[:].bitcast(U16).rearrange("p (j d) -> p d j", d=2))
+
+        def tab_operand(a, c, j0, width):
+            codes = tab_codes[c][:, a, j0 : j0 + width].bitcast(U8).bitcast(FP4X4)
+            plane = picked_scales[:] if a == 0 else second_scales[:].bitcast(U8)
+            return codes, plane[:, CHUNK * c + j0 : CHUNK * c + j0 + width]
+
+        def wide_product(lhs_c, lhs_s, m0, rhs_of_pass):
+            bank = psum.tile([P, 512], F32, name="bank", tag="bank")
+            for a in range(2):
+                codes, scales = rhs_of_pass(a)
+                nc.tensor.matmul_mx(
+                    out=bank[:],
+                    lhsT=lhs_c[a][:, m0 : m0 + P].bitcast(FP8X4),
+                    lhsT_scale=lhs_s[a][:, m0 : m0 + P],
+                    rhs=codes,
+                    rhs_scale=scales,
+                    start=(a == 0),
+                    stop=(a == 1),
+                )
+            return bank
+
+        def feature_product(w_c, w_s, b, rhs_of_pass):
+            bank = psum.tile([P, 512], F32, name="bank", tag="bank")
+            for t in range(4):
+                m0 = PASS * b + P * t
+                for a in range(2):
+                    codes, scales = rhs_of_pass(a)
+                    nc.tensor.matmul_mx(
+                        out=bank[:, P * t : P * (t + 1)],
+                        lhsT=w_c[a][:, m0 : m0 + P].bitcast(FP8X4),
+                        lhsT_scale=w_s[a][:, m0 : m0 + P],
+                        rhs=codes,
+                        rhs_scale=scales,
+                        start=(a == 0),
+                        stop=(a == 1),
+                    )
+            return bank
+
+        def relu_out(engine, out, bank):
+            view_out = out.rearrange("p (j t) -> p j t", t=4)
+            view_in = bank[:].rearrange("p (t j) -> p j t", t=4)
+            if engine == "scalar":
+                nc.scalar.activation(view_out, view_in, RELU)
+            else:
+                nc.vector.tensor_scalar(view_out, view_in, 0.0, None, MAX)
+
+        def scale_out(engine, out, bank, factor):
+            if engine == "scalar":
+                nc.scalar.activation(out, bank[:], COPY, scale=factor)
+            else:
+                nc.vector.tensor_scalar(out, bank[:], factor, None, MULT)
+
+        gather_scales(0)
+        picked = gather_words(0)
+        for a in range(2):
+            quantize(wv_c[a], wv_s[a], 0, 256, round_plain("scalar", wv_raw[a, 0], 256)[:, 0:1024])
+        part_words(0, picked)
+        part_words(1, gather_words(1))
+        for a in range(2):
+            quantize(wv_c[a], wv_s[a], 256, 256, round_plain("scalar", wv_raw[a, 1], 256)[:, 0:1024])
+        gather_scales(1)
+        part_words(2, gather_words(2))
+        part_words(3, gather_words(3))
+
+        def values(pair, half):
+            for nt in (2 * half, 2 * half + 1):
+                staged = ring.tile([P, 1024], F32, name="staged", tag="staged", bufs=10)
+                for i in range(2):
+                    c = 2 * pair + i
+                    bank = wide_product(wv_c, wv_s, P * nt, lambda a: tab_operand(a, c, 0, CHUNK))
+                    nc.scalar.copy(staged[:, 512 * i : 512 * (i + 1)], bank[:])
+                stores.append((out_1[P * nt : P * (nt + 1), 1024 * pair : 1024 * (pair + 1)], staged))
+
+        stores = []
+        values(0, 0)
+        values(0, 1)
+        for a, engine in ((0, "scalar"), (1, "vector")):
+            quantize(wk_c[a], wk_s[a], 0, 512, round_permuted(engine, wk_raw[a, 0])[:])
+        wq_raw = {(a, b): load(wq, a, 512 * b, 512, "raw", 6) for a, b in ((0, 0), (1, 0))}
+        values(1, 0)
+        values(1, 1)
+        for a in range(2):
+            quantize(wk_c[a], wk_s[a], 512, 512, round_permuted("vector", wk_raw[a, 1])[:])
+        for a in range(2):
+            wq_raw[a, 1] = load(wq, a, 512, 512, "raw", 6)
+        for dst, staged in stores:
+            nc.sync.dma_start(dst, staged[:])
+
+        def keys(b, c):
+            rounded = ring.tile([P, 2048], BF16, name="rounded", tag="rounded", bufs=3, align_bytes=64)
+            for s in range(4):
+                bank = feature_product(wk_c, wk_s, b, lambda a: tab_operand(a, c, P * s, P))
+                relu_out("scalar", rounded[:, 512 * s : 512 * (s + 1)], bank)
+            quantize(ka_c[b], ka_s[b], CHUNK * c, CHUNK, rounded[:])
+
+        def queries(mt):
+            for b in range(2):
+                rounded = ring.tile([P, 512], BF16, name="rounded_q", tag="rounded_q", bufs=3, align_bytes=64)
+                bank = feature_product(
+                    wq_c, wq_s, b, lambda a: (x_c[a][:, P * mt : P * (mt + 1)].bitcast(FP8X4), x_s[a][:, P * mt : P * (mt + 1)])
+                )
+                relu_out("scalar" if b == 0 else "vector", rounded[:], bank)
+                quantize(qa_c[b], qa_s[b], P * mt, P, rounded[:])
+
+        def scores(mt, chunks):
+            staged = ring.tile([P, 1024], F32, name="staged", tag="staged", bufs=10)
+            for i, c in enumerate(chunks):
+                cols = slice(CHUNK * c, CHUNK * (c + 1))
+                bank = wide_product(qa_c, qa_s, P * mt, lambda b: (ka_c[b][:, cols].bitcast(FP8X4), ka_s[b][:, cols]))
+                scale_out("scalar" if (mt + c) % 2 == 0 else "vector", staged[:, 512 * i : 512 * (i + 1)], bank, SCORE_SCALE)
+            width = CHUNK * len(chunks)
+            nc.sync.dma_start(
+                out_0[P * mt : P * (mt + 1), CHUNK * chunks[0] : CHUNK * chunks[0] + width], staged[:, 0:width]
+            )
+
+        keys(0, 0)
+        keys(0, 1)
+        for a in range(2):
+            quantize(x_c[a], x_s[a], 0, 512, round_plain("vector", x_raw[a], 512)[:])
+        keys(0, 2)
+        keys(0, 3)
+        for a in range(2):
+            quantize(wq_c[a], wq_s[a], 0, 512, round_permuted("vector", wq_raw[a, 0])[:])
+        keys(1, 0)
+        for a in range(2):
+            quantize(wq_c[a], wq_s[a], 512, 512, round_permuted("vector", wq_raw[a, 1])[:])
+        keys(1, 1)
+        for mt in range(4):
+            queries(mt)
+        keys(1, 2)
+        for mt in range(4):
+            scores(mt, (0, 1))
+        keys(1, 3)
+        for c in (2, 3):
+            for mt in range(4):
+                scores(mt, (c,))

@@ -35,7 +35,6 @@ def tile_list_kvt_act_kernel(
 
         offsets = keep.tile([P, J // 16], U16, name="offsets")
         table_words = keep.tile([P, T], I32, name="table_words")
-        table_scales = keep.tile([P, T // 4], I32, name="table_scales")
         picked_scales = keep.tile([P, J], U8, name="picked_scales", align_bytes=64)
         second_scales = keep.tile([P, J // 4], I32, name="second_scales", align_bytes=64)
         tab_codes = [keep.tile([P, 2, CHUNK], U16, name="tab_codes%d" % c, align_bytes=64) for c in range(4)]
@@ -53,22 +52,11 @@ def tile_list_kvt_act_kernel(
         qa_c, qa_s = codes_pair("qa", M)
         ka_c, ka_s = codes_pair("ka", J)
 
-        nc.vector.memset(table_scales[:], 0)
-        nc.vector.memset(second_scales[:], 0)
-        nc.sync.dma_start(offsets[:], offs)
-        nc.sync.dma_start(table_words[:], tab_words[0].rearrange("p t b -> p (t b)").bitcast(I32))
-        rows = tab_scales.bitcast(I32).rearrange("a (q r) t -> r q a t", r=4)
-        for r in range(4):
-            nc.scalar.dma_start(table_scales[r:P:16, :], rows[r])
-
-        def load(w, a, c0, width, tag, bufs):
-            raw = ring.tile([P, 4, width], F32, name=tag, tag=tag, bufs=bufs)
+        def load(pool, w, a, c0, width, tag, bufs):
+            raw = pool.tile([P, 4, width], F32, name=tag, tag=tag, bufs=bufs)
             nc.sync.dma_start(raw[:], w[PASS * a : PASS * (a + 1), c0 : c0 + width].rearrange("(p j) c -> p j c", j=4))
             return raw
 
-        wv_raw = {(a, h): load(wv, a, 256 * h, 256, "raw_half", 4) for h in range(2) for a in range(2)}
-        wk_raw = {(a, b): load(wk, a, 512 * b, 512, "raw", 6) for b in range(2) for a in range(2)}
-        x_raw = {a: load(x, a, 0, 512, "raw", 6) for a in range(2)}
 
         def copy_on(engine, out, in_):
             if engine == "scalar":
@@ -76,8 +64,8 @@ def tile_list_kvt_act_kernel(
             else:
                 nc.vector.tensor_copy(out, in_)
 
-        def round_plain(engine, raw, width):
-            grouped = ring.tile([P, 4 * width], BF16, name="grouped", tag="grouped", bufs=4, align_bytes=64)
+        def round_plain(engine, raw, width, tag="grouped", bufs=4):
+            grouped = ring.tile([P, 4 * width], BF16, name="grouped", tag=tag, bufs=bufs, align_bytes=64)
             copy_on(
                 engine,
                 grouped[:].rearrange("p (c i j) -> p c j i", i=4, j=4),
@@ -99,16 +87,16 @@ def tile_list_kvt_act_kernel(
                 out=codes[:, c0 : c0 + width].bitcast(FP8X4), scales=scales[:, c0 : c0 + width], in_=grouped
             )
 
-        def gather_scales(h):
+        def gather_scales(table_scales, h):
             cols = slice(1024 * h, 1024 * (h + 1))
             nc.vector.tensor_copy(
                 picked_scales[:, cols], table_scales[:].bitcast(U8).indirect(offsets[:, 64 * h : 64 * (h + 1)])
             )
             words = slice(256 * h, 256 * (h + 1))
-            nc.scalar.dma_start(second_scales[0:112, words], picked_scales[16:P, :].bitcast(I32)[:, words])
+            nc.scalar.dma_start(second_scales[0:100, words], picked_scales[28:P, :].bitcast(I32)[:, words])
 
         def gather_words(c):
-            picked = ring.tile([P, CHUNK], U32, name="picked", tag="picked", bufs=2)
+            picked = ring.tile([P, CHUNK], U32, name="picked", tag="slot%d" % c, bufs=1, align_bytes=64)
             nc.vector.tensor_copy(picked[:], table_words[:].bitcast(U32).indirect(offsets[:, 32 * c : 32 * (c + 1)]))
             return picked
 
@@ -166,42 +154,6 @@ def tile_list_kvt_act_kernel(
             else:
                 nc.vector.tensor_scalar(out, bank[:], factor, None, MULT)
 
-        gather_scales(0)
-        picked = gather_words(0)
-        for a in range(2):
-            quantize(wv_c[a], wv_s[a], 0, 256, round_plain("scalar", wv_raw[a, 0], 256)[:, 0:1024])
-        part_words(0, picked)
-        part_words(1, gather_words(1))
-        for a in range(2):
-            quantize(wv_c[a], wv_s[a], 256, 256, round_plain("scalar", wv_raw[a, 1], 256)[:, 0:1024])
-        gather_scales(1)
-        part_words(2, gather_words(2))
-        part_words(3, gather_words(3))
-
-        def values(pair, half):
-            for nt in (2 * half, 2 * half + 1):
-                staged = ring.tile([P, 1024], F32, name="staged", tag="staged", bufs=10)
-                for i in range(2):
-                    c = 2 * pair + i
-                    bank = wide_product(wv_c, wv_s, P * nt, lambda a: tab_operand(a, c, 0, CHUNK))
-                    nc.scalar.copy(staged[:, 512 * i : 512 * (i + 1)], bank[:])
-                stores.append((out_1[P * nt : P * (nt + 1), 1024 * pair : 1024 * (pair + 1)], staged))
-
-        stores = []
-        values(0, 0)
-        values(0, 1)
-        for a, engine in ((0, "scalar"), (1, "vector")):
-            quantize(wk_c[a], wk_s[a], 0, 512, round_permuted(engine, wk_raw[a, 0])[:])
-        wq_raw = {(a, b): load(wq, a, 512 * b, 512, "raw", 6) for a, b in ((0, 0), (1, 0))}
-        values(1, 0)
-        values(1, 1)
-        for a in range(2):
-            quantize(wk_c[a], wk_s[a], 512, 512, round_permuted("vector", wk_raw[a, 1])[:])
-        for a in range(2):
-            wq_raw[a, 1] = load(wq, a, 512, 512, "raw", 6)
-        for dst, staged in stores:
-            nc.sync.dma_start(dst, staged[:])
-
         def keys(b, c):
             rounded = ring.tile([P, 2048], BF16, name="rounded", tag="rounded", bufs=3, align_bytes=64)
             for s in range(4):
@@ -229,24 +181,85 @@ def tile_list_kvt_act_kernel(
                 out_0[P * mt : P * (mt + 1), CHUNK * chunks[0] : CHUNK * chunks[0] + width], staged[:, 0:width]
             )
 
+
+        def values(nt, pair, engines):
+            staged = ring.tile([P, 1024], F32, name="staged", tag="staged", bufs=10)
+            for i in range(2):
+                c = 2 * pair + i
+                bank = wide_product(wv_c, wv_s, P * nt, lambda a: tab_operand(a, c, 0, CHUNK))
+                copy_on(engines[i], staged[:, 512 * i : 512 * (i + 1)], bank[:])
+            stores.append((out_1[P * nt : P * (nt + 1), 1024 * pair : 1024 * (pair + 1)], staged))
+
+        def wv_piece(i):
+            c0, width = wv_pieces[i]
+            quantize(wv_c[0], wv_s[0], c0, width, round_plain("scalar", wv_raw[0, c0], width)[:])
+            quantize(wv_c[1], wv_s[1], c0, width, round_plain("scalar", wv_raw[1, c0], width, "slot%d" % (i + 1), 1)[:])
+
+        def feature_weights(codes, scales, raw, b, engines):
+            for a in range(2):
+                quantize(codes[a], scales[a], 512 * b, 512, round_permuted(engines[a], raw[a, b])[:])
+
+        stores = []
+        wv_pieces = ((0, 128), (128, 128), (256, 256))
+        with tc.tile_pool(name="early", bufs=1) as early:
+            table_scales = early.tile([P, T // 4], I32, name="table_scales")
+            nc.vector.memset(second_scales[:], 0)
+            nc.sync.dma_start(offsets[:], offs)
+            rows = tab_scales.rearrange("a q t -> (a q) t").bitcast(I32)
+            for g in range(8):
+                first = 4 * (g // 2) + 4 * (g % 2)
+                nc.sync.dma_start(table_scales[16 * g : 16 * (g + 1), :], rows[first : first + 16, :])
+            nc.sync.dma_start(table_words[:], tab_words[0].rearrange("p t b -> p (t b)").bitcast(I32))
+            wv_raw = {
+                (a, c0): load(ring, wv, a, c0, width, "raw_wv%d_%d" % (a, c0), 1)
+                for c0, width in wv_pieces[:2]
+                for a in range(2)
+            }
+            gather_scales(table_scales, 0)
+            gather_scales(table_scales, 1)
+
+        late = ctx.enter_context(tc.tile_pool(name="late", bufs=1))
+        for a in range(2):
+            wv_raw[a, 256] = load(late, wv, a, 256, 256, "raw_half", 2)
+        wk_raw = {(a, b): load(late, wk, a, 512 * b, 512, "raw", 6) for b in range(2) for a in range(2)}
+        x_raw = {a: load(late, x, a, 0, 512, "raw", 6) for a in range(2)}
+        part_words(0, gather_words(0))
+        for i in range(3):
+            wv_piece(i)
+            part_words(i + 1, gather_words(i + 1))
+
+        both_scalar = ("scalar", "scalar")
+        both_vector = ("vector", "vector")
+        for nt in range(4):
+            values(nt, 0, both_scalar)
+        feature_weights(wk_c, wk_s, wk_raw, 0, ("scalar", "vector"))
+        wq_raw = {(a, 0): load(late, wq, a, 0, 512, "raw", 6) for a in range(2)}
+        for nt in range(4):
+            values(nt, 1, both_scalar)
         keys(0, 0)
+        feature_weights(wk_c, wk_s, wk_raw, 1, both_vector)
+        for a in range(2):
+            wq_raw[a, 1] = load(late, wq, a, 512, 512, "raw", 6)
+        for dst, staged in stores:
+            nc.sync.dma_start(dst, staged[:])
         keys(0, 1)
+        keys(0, 2)
         for a in range(2):
             quantize(x_c[a], x_s[a], 0, 512, round_plain("vector", x_raw[a], 512)[:])
-        keys(0, 2)
         keys(0, 3)
-        for a in range(2):
-            quantize(wq_c[a], wq_s[a], 0, 512, round_permuted("vector", wq_raw[a, 0])[:])
         keys(1, 0)
-        for a in range(2):
-            quantize(wq_c[a], wq_s[a], 512, 512, round_permuted("vector", wq_raw[a, 1])[:])
+        feature_weights(wq_c, wq_s, wq_raw, 0, both_vector)
         keys(1, 1)
-        for mt in range(4):
-            queries(mt)
         keys(1, 2)
-        for mt in range(4):
-            scores(mt, (0, 1))
+        feature_weights(wq_c, wq_s, wq_raw, 1, both_vector)
         keys(1, 3)
-        for c in (2, 3):
-            for mt in range(4):
-                scores(mt, (c,))
+        queries(0)
+        queries(1)
+        for mt in range(4):
+            if mt < 2:
+                queries(mt + 2)
+            scores(mt, (0, 1))
+            if mt < 3:
+                scores(mt, (2, 3))
+        scores(3, (2,))
+        scores(3, (3,))

@@ -52,11 +52,9 @@ def tile_list_kvt_act_kernel(
         qa_c, qa_s = codes_pair("qa", M)
         ka_c, ka_s = codes_pair("ka", J)
 
-        def load(pool, w, a, c0, width, tag, bufs):
-            raw = pool.tile([P, 4, width], F32, name=tag, tag=tag, bufs=bufs)
-            nc.sync.dma_start(raw[:], w[PASS * a : PASS * (a + 1), c0 : c0 + width].rearrange("(p j) c -> p j c", j=4))
+        def load(raw, w, a, c0, width):
+            nc.sync.dma_start(raw, w[PASS * a : PASS * (a + 1), c0 : c0 + width].rearrange("(p j) c -> p j c", j=4))
             return raw
-
 
         def copy_on(engine, out, in_):
             if engine == "scalar":
@@ -64,21 +62,21 @@ def tile_list_kvt_act_kernel(
             else:
                 nc.vector.tensor_copy(out, in_)
 
-        def round_plain(engine, raw, width, tag="grouped", bufs=4):
-            grouped = ring.tile([P, 4 * width], BF16, name="grouped", tag=tag, bufs=bufs, align_bytes=64)
+        def round_plain(engine, raw, width, slot):
+            grouped = ring.tile([P, 4 * width], BF16, name="grouped", tag="slot%d" % slot, align_bytes=64)
             copy_on(
                 engine,
                 grouped[:].rearrange("p (c i j) -> p c j i", i=4, j=4),
-                raw[:].rearrange("p j (c i) -> p c j i", i=4),
+                raw.rearrange("p j (c i) -> p c j i", i=4),
             )
             return grouped
 
-        def round_permuted(engine, raw):
-            grouped = ring.tile([P, 2048], BF16, name="grouped", tag="grouped", bufs=4, align_bytes=64)
+        def round_permuted(engine, raw, slot):
+            grouped = ring.tile([P, 2048], BF16, name="grouped", tag="slot%d" % slot, align_bytes=64)
             copy_on(
                 engine,
                 grouped[:].rearrange("p (t c i j) -> p t c j i", t=4, i=4, j=4),
-                raw[:].rearrange("p j (c t i) -> p t c j i", t=4, i=4),
+                raw.rearrange("p j (c t i) -> p t c j i", t=4, i=4),
             )
             return grouped
 
@@ -93,10 +91,11 @@ def tile_list_kvt_act_kernel(
                 picked_scales[:, cols], table_scales[:].bitcast(U8).indirect(offsets[:, 64 * h : 64 * (h + 1)])
             )
             words = slice(256 * h, 256 * (h + 1))
-            nc.scalar.dma_start(second_scales[0:100, words], picked_scales[28:P, :].bitcast(I32)[:, words])
+            nc.scalar.dma_start(second_scales[0:4, words], picked_scales[16:20, :].bitcast(I32)[:, words])
+            nc.scalar.dma_start(second_scales[32:100, words], picked_scales[60:P, :].bitcast(I32)[:, words])
 
-        def gather_words(c):
-            picked = ring.tile([P, CHUNK], U32, name="picked", tag="slot%d" % c, bufs=1, align_bytes=64)
+        def gather_words(c, slot):
+            picked = ring.tile([P, CHUNK], U32, name="picked", tag="slot%d" % slot, align_bytes=64)
             nc.vector.tensor_copy(picked[:], table_words[:].bitcast(U32).indirect(offsets[:, 32 * c : 32 * (c + 1)]))
             return picked
 
@@ -108,8 +107,8 @@ def tile_list_kvt_act_kernel(
             plane = picked_scales[:] if a == 0 else second_scales[:].bitcast(U8)
             return codes, plane[:, CHUNK * c + j0 : CHUNK * c + j0 + width]
 
-        def wide_product(lhs_c, lhs_s, m0, rhs_of_pass):
-            bank = psum.tile([P, 512], F32, name="bank", tag="bank")
+        def wide_product(lhs_c, lhs_s, m0, rhs_of_pass, width=512):
+            bank = psum.tile([P, width], F32, name="bank", tag="bank")
             for a in range(2):
                 codes, scales = rhs_of_pass(a)
                 nc.tensor.matmul_mx(
@@ -154,11 +153,14 @@ def tile_list_kvt_act_kernel(
             else:
                 nc.vector.tensor_scalar(out, bank[:], factor, None, MULT)
 
-        def keys(b, c):
-            rounded = ring.tile([P, 2048], BF16, name="rounded", tag="rounded", bufs=3, align_bytes=64)
+        def keys(b, c, slot, on_vector=()):
+            rounded = ring.tile([P, 2048], BF16, name="rounded", tag="slot%d" % slot, align_bytes=64)
             for s in range(4):
                 bank = feature_product(wk_c, wk_s, b, lambda a: tab_operand(a, c, P * s, P))
-                relu_out("scalar", rounded[:, 512 * s : 512 * (s + 1)], bank)
+                relu_out("vector" if s in on_vector else "scalar", rounded[:, 512 * s : 512 * (s + 1)], bank)
+            return rounded
+
+        def quantize_keys(b, c, rounded):
             quantize(ka_c[b], ka_s[b], CHUNK * c, CHUNK, rounded[:])
 
         def queries(mt):
@@ -167,99 +169,126 @@ def tile_list_kvt_act_kernel(
                 bank = feature_product(
                     wq_c, wq_s, b, lambda a: (x_c[a][:, P * mt : P * (mt + 1)].bitcast(FP8X4), x_s[a][:, P * mt : P * (mt + 1)])
                 )
-                relu_out("scalar" if b == 0 else "vector", rounded[:], bank)
+                relu_out("vector" if mt < 1 or b == 1 else "scalar", rounded[:], bank)
                 quantize(qa_c[b], qa_s[b], P * mt, P, rounded[:])
 
-        def scores(mt, chunks):
-            staged = ring.tile([P, 1024], F32, name="staged", tag="staged", bufs=10)
-            for i, c in enumerate(chunks):
-                cols = slice(CHUNK * c, CHUNK * (c + 1))
-                bank = wide_product(qa_c, qa_s, P * mt, lambda b: (ka_c[b][:, cols].bitcast(FP8X4), ka_s[b][:, cols]))
-                scale_out("scalar" if (mt + c) % 2 == 0 else "vector", staged[:, 512 * i : 512 * (i + 1)], bank, SCORE_SCALE)
-            width = CHUNK * len(chunks)
-            nc.sync.dma_start(
-                out_0[P * mt : P * (mt + 1), CHUNK * chunks[0] : CHUNK * chunks[0] + width], staged[:, 0:width]
-            )
+        def scores(mt, c, staged):
+            cols = slice(CHUNK * c, CHUNK * (c + 1))
+            bank = wide_product(qa_c, qa_s, P * mt, lambda b: (ka_c[b][:, cols].bitcast(FP8X4), ka_s[b][:, cols]))
+            scale_out("scalar" if (mt + c) % 2 == 0 else "vector", staged[:, cols], bank, SCORE_SCALE)
 
 
-        def values(nt, pair, engines):
-            staged = ring.tile([P, 1024], F32, name="staged", tag="staged", bufs=10)
-            for i in range(2):
-                c = 2 * pair + i
-                bank = wide_product(wv_c, wv_s, P * nt, lambda a: tab_operand(a, c, 0, CHUNK))
-                copy_on(engines[i], staged[:, 512 * i : 512 * (i + 1)], bank[:])
-            stores.append((out_1[P * nt : P * (nt + 1), 1024 * pair : 1024 * (pair + 1)], staged))
+        def values(nt, c):
+            bank = wide_product(wv_c, wv_s, P * nt, lambda a: tab_operand(a, c, 0, CHUNK))
+            nc.scalar.copy(value_rows[nt][:, CHUNK * c : CHUNK * (c + 1)], bank[:])
 
-        def wv_piece(i):
-            c0, width = wv_pieces[i]
-            quantize(wv_c[0], wv_s[0], c0, width, round_plain("scalar", wv_raw[0, c0], width)[:])
-            quantize(wv_c[1], wv_s[1], c0, width, round_plain("scalar", wv_raw[1, c0], width, "slot%d" % (i + 1), 1)[:])
+        def wv_piece(a, c0, width, slot):
+            raw = wv_raw[a, c0 // 256][:, :, c0 % 256 : c0 % 256 + width]
+            quantize(wv_c[a], wv_s[a], c0, width, round_plain("scalar", raw, width, slot)[:])
 
-        def feature_weights(codes, scales, raw, b, engines):
-            for a in range(2):
-                quantize(codes[a], scales[a], 512 * b, 512, round_permuted(engines[a], raw[a, b])[:])
+        def feature_weights(codes, scales, raw, a, b, engine, slot):
+            quantize(codes[a], scales[a], 512 * b, 512, round_permuted(engine, raw, slot)[:])
 
-        stores = []
-        wv_pieces = ((0, 128), (128, 128), (256, 256))
         with tc.tile_pool(name="early", bufs=1) as early:
             table_scales = early.tile([P, T // 4], I32, name="table_scales")
             nc.vector.memset(second_scales[:], 0)
+            warm_in = keep.tile([P, 8], F32, name="warm_in")
+            warm_out = keep.tile([P, 8], F32, name="warm_out")
+            nc.vector.memset(warm_in[:], 0.0)
+            nc.scalar.activation(warm_out[:], warm_in[:], RELU)
             nc.sync.dma_start(offsets[:], offs)
             rows = tab_scales.rearrange("a q t -> (a q) t").bitcast(I32)
-            for g in range(8):
+            nc.sync.dma_start(table_scales[0:32, :], rows)
+            for g in range(2, 8):
                 first = 4 * (g // 2) + 4 * (g % 2)
                 nc.sync.dma_start(table_scales[16 * g : 16 * (g + 1), :], rows[first : first + 16, :])
             nc.sync.dma_start(table_words[:], tab_words[0].rearrange("p t b -> p (t b)").bitcast(I32))
             wv_raw = {
-                (a, c0): load(ring, wv, a, c0, width, "raw_wv%d_%d" % (a, c0), 1)
-                for c0, width in wv_pieces[:2]
-                for a in range(2)
+                (a, 0): load(ring.tile([P, 4, 256], F32, name="wv_low%d" % a)[:], wv, a, 0, 256) for a in range(2)
             }
             gather_scales(table_scales, 0)
             gather_scales(table_scales, 1)
 
         late = ctx.enter_context(tc.tile_pool(name="late", bufs=1))
         for a in range(2):
-            wv_raw[a, 256] = load(late, wv, a, 256, 256, "raw_half", 2)
-        wk_raw = {(a, b): load(late, wk, a, 512 * b, 512, "raw", 6) for b in range(2) for a in range(2)}
-        x_raw = {a: load(late, x, a, 0, 512, "raw", 6) for a in range(2)}
-        part_words(0, gather_words(0))
-        for i in range(3):
-            wv_piece(i)
-            part_words(i + 1, gather_words(i + 1))
+            wv_raw[a, 1] = load(late.tile([P, 4, 256], F32, name="wv_high%d" % a)[:], wv, a, 256, 256)
+        wk_raw = {}
+        for b in range(2):
+            pair = late.tile([P, 2, 4, 512], F32, name="raw", tag="raw%d" % b)
+            for a in range(2):
+                wk_raw[a, b] = load(pair[:, a], wk, a, 512 * b, 512)
 
-        both_scalar = ("scalar", "scalar")
-        both_vector = ("vector", "vector")
+        part_words(0, gather_words(0, 0))
+        wv_piece(0, 0, 256, 4)
+        wv_piece(1, 0, 128, 5)
+        part_words(1, gather_words(1, 2))
+        wv_piece(1, 128, 128, 6)
+        part_words(2, gather_words(2, 5))
+        wv_piece(0, 256, 256, 4)
+        part_words(3, gather_words(3, 6))
+        wv_piece(1, 256, 256, 1)
+
+        value_rows = [ring.tile([P, J], F32, name="staged", tag="staged%d" % nt) for nt in range(4)]
         for nt in range(4):
-            values(nt, 0, both_scalar)
-        feature_weights(wk_c, wk_s, wk_raw, 0, ("scalar", "vector"))
-        wq_raw = {(a, 0): load(late, wq, a, 0, 512, "raw", 6) for a in range(2)}
+            values(nt, 0)
+            values(nt, 1)
+        feature_weights(wk_c, wk_s, wk_raw[0, 0], 0, 0, "vector", 4)
+        feature_weights(wk_c, wk_s, wk_raw[1, 0], 1, 0, "vector", 4)
+        pair = late.tile([P, 2, 4, 512], F32, name="raw", tag="raw2")
+        x_raw = [load(pair[:, a], x, a, 0, M) for a in range(2)]
+        wq_raw = {}
+        for b, tag in enumerate(("raw3", "raw0")):
+            pair = late.tile([P, 2, 4, 512], F32, name="raw", tag=tag)
+            for a in range(2):
+                wq_raw[a, b] = load(pair[:, a], wq, a, 512 * b, 512)
+        for c in (2, 3):
+            for nt in range(4):
+                values(nt, c)
+        feature_weights(wk_c, wk_s, wk_raw[0, 1], 0, 1, "vector", 4)
+        feature_weights(wk_c, wk_s, wk_raw[1, 1], 1, 1, "vector", 4)
         for nt in range(4):
-            values(nt, 1, both_scalar)
-        keys(0, 0)
-        feature_weights(wk_c, wk_s, wk_raw, 1, both_vector)
-        for a in range(2):
-            wq_raw[a, 1] = load(late, wq, a, 512, 512, "raw", 6)
-        for dst, staged in stores:
-            nc.sync.dma_start(dst, staged[:])
-        keys(0, 1)
-        keys(0, 2)
-        for a in range(2):
-            quantize(x_c[a], x_s[a], 0, 512, round_plain("vector", x_raw[a], 512)[:])
-        keys(0, 3)
-        keys(1, 0)
-        feature_weights(wq_c, wq_s, wq_raw, 0, both_vector)
-        keys(1, 1)
-        keys(1, 2)
-        feature_weights(wq_c, wq_s, wq_raw, 1, both_vector)
-        keys(1, 3)
+            nc.sync.dma_start(out_1[P * nt : P * (nt + 1), :], value_rows[nt][:])
+        quantize_keys(0, 0, keys(0, 0, 0))
+        quantize(x_c[0], x_s[0], 0, M, round_plain("vector", x_raw[0], M, 4)[:])
+        quantize_keys(0, 1, keys(0, 1, 1))
+        quantize(x_c[1], x_s[1], 0, M, round_plain("vector", x_raw[1], M, 0)[:])
+        quantize_keys(0, 2, keys(0, 2, 2))
+        feature_weights(wq_c, wq_s, wq_raw[0, 0], 0, 0, "vector", 4)
+        quantize_keys(0, 3, keys(0, 3, 3))
+        feature_weights(wq_c, wq_s, wq_raw[1, 0], 1, 0, "vector", 0)
+        held = [keys(1, 0, 5)]
+        feature_weights(wq_c, wq_s, wq_raw[0, 1], 0, 1, "vector", 4)
+        quantize_keys(1, 0, held[0])
+        held.append(keys(1, 1, 6))
+        feature_weights(wq_c, wq_s, wq_raw[1, 1], 1, 1, "vector", 0)
+        quantize_keys(1, 1, held[1])
+        held.append(keys(1, 2, 7))
+        held.append(keys(1, 3, 8))
         queries(0)
+        quantize_keys(1, 2, held[2])
+        quantize_keys(1, 3, held[3])
         queries(1)
         for mt in range(4):
             if mt < 2:
                 queries(mt + 2)
-            scores(mt, (0, 1))
+            staged = ring.tile([P, J], F32, name="staged", tag="staged%d" % mt)
+            out_rows = out_0[P * mt : P * (mt + 1), :]
             if mt < 3:
-                scores(mt, (2, 3))
-        scores(3, (2,))
-        scores(3, (3,))
+                for c in range(4):
+                    scores(mt, c, staged)
+                    if c % 2 == 1:
+                        cols = slice(CHUNK * (c - 1), CHUNK * (c + 1))
+                        nc.sync.dma_start(out_rows[:, cols], staged[:, cols])
+            else:
+                scores(mt, 0, staged)
+                scores(mt, 1, staged)
+                nc.sync.dma_start(out_rows[:, 0:1024], staged[:, 0:1024])
+                scores(mt, 2, staged)
+                nc.sync.dma_start(out_rows[:, 1024:1536], staged[:, 1024:1536])
+                for half, engine in enumerate(("vector", "scalar")):
+                    cols = slice(J - 512 + 256 * half, J - 256 + 256 * half)
+                    bank = wide_product(
+                        qa_c, qa_s, P * mt, lambda b: (ka_c[b][:, cols].bitcast(FP8X4), ka_s[b][:, cols]), 256
+                    )
+                    scale_out(engine, staged[:, cols], bank, SCORE_SCALE)
+                    nc.sync.dma_start(out_rows[:, cols], staged[:, cols])

@@ -34,7 +34,8 @@ def tile_list_kvt_act_kernel(
         psum = ctx.enter_context(tc.psum_pool(name="psum", bufs=8))
 
         offsets = keep.tile([P, J // 16], U16, name="offsets")
-        table_words = keep.tile([P, T], I32, name="table_words")
+        arena = ctx.enter_context(tc.tile_pool(name="arena", bufs=1))
+        table_words = arena.tile([P, T], I32, name="table_words", offset=0, align_bytes=64)
         picked_scales = keep.tile([P, J], U8, name="picked_scales", align_bytes=64)
         second_scales = keep.tile([P, J // 4], I32, name="second_scales", align_bytes=64)
         tab_codes = [keep.tile([P, 2, CHUNK], U16, name="tab_codes%d" % c, align_bytes=64) for c in range(4)]
@@ -50,33 +51,32 @@ def tile_list_kvt_act_kernel(
         wq_c, wq_s = codes_pair("wq", R)
         x_c, x_s = codes_pair("x", M)
         qa_c, qa_s = codes_pair("qa", M)
-        ka_c, ka_s = codes_pair("ka", J)
+        ka_c = [keep.tile([P, J], U32, name="ka_codes%d" % b, align_bytes=64) for b in range(2)]
+        ka_early_scales = keep.tile([P, CHUNK], U8, name="ka_early_scales", align_bytes=64)
 
         def load(raw, w, a, c0, width):
             nc.sync.dma_start(raw, w[PASS * a : PASS * (a + 1), c0 : c0 + width].rearrange("(p j) c -> p j c", j=4))
             return raw
 
-        def copy_on(engine, out, in_):
+        def staging(dtype, width, tag):
+            bufs = 4 if tag == "cast" else 1
+            return ring.tile([P, width], dtype, name="staging", tag=tag, bufs=bufs, align_bytes=64)
+
+        def round_plain(engine, raw, width, tag):
+            grouped = staging(BF16, 4 * width, tag)
+            out = grouped[:].rearrange("p (c i j) -> p c j i", i=4, j=4)
+            in_ = raw.rearrange("p j (c i) -> p c j i", i=4)
             if engine == "scalar":
                 nc.scalar.copy(out, in_)
             else:
                 nc.vector.tensor_copy(out, in_)
-
-        def round_plain(engine, raw, width, slot):
-            grouped = ring.tile([P, 4 * width], BF16, name="grouped", tag="slot%d" % slot, align_bytes=64)
-            copy_on(
-                engine,
-                grouped[:].rearrange("p (c i j) -> p c j i", i=4, j=4),
-                raw.rearrange("p j (c i) -> p c j i", i=4),
-            )
             return grouped
 
-        def round_permuted(engine, raw, slot):
-            grouped = ring.tile([P, 2048], BF16, name="grouped", tag="slot%d" % slot, align_bytes=64)
-            copy_on(
-                engine,
-                grouped[:].rearrange("p (t c i j) -> p t c j i", t=4, i=4, j=4),
-                raw.rearrange("p j (c t i) -> p t c j i", t=4, i=4),
+        def round_permuted(raw, half):
+            grouped = staging(BF16, 1024, "cast")
+            nc.vector.tensor_copy(
+                grouped[:].rearrange("p (t c i j) -> p t c j i", t=2, i=4, j=4),
+                raw.rearrange("p j (c t i) -> p t c j i", t=4, i=4)[:, 2 * half : 2 * half + 2],
             )
             return grouped
 
@@ -85,17 +85,8 @@ def tile_list_kvt_act_kernel(
                 out=codes[:, c0 : c0 + width].bitcast(FP8X4), scales=scales[:, c0 : c0 + width], in_=grouped
             )
 
-        def gather_scales(table_scales, h):
-            cols = slice(1024 * h, 1024 * (h + 1))
-            nc.vector.tensor_copy(
-                picked_scales[:, cols], table_scales[:].bitcast(U8).indirect(offsets[:, 64 * h : 64 * (h + 1)])
-            )
-            words = slice(256 * h, 256 * (h + 1))
-            nc.scalar.dma_start(second_scales[0:4, words], picked_scales[16:20, :].bitcast(I32)[:, words])
-            nc.scalar.dma_start(second_scales[32:100, words], picked_scales[60:P, :].bitcast(I32)[:, words])
-
-        def gather_words(c, slot):
-            picked = ring.tile([P, CHUNK], U32, name="picked", tag="slot%d" % slot, align_bytes=64)
+        def gather_words(c, tag):
+            picked = staging(U32, CHUNK, tag)
             nc.vector.tensor_copy(picked[:], table_words[:].bitcast(U32).indirect(offsets[:, 32 * c : 32 * (c + 1)]))
             return picked
 
@@ -153,41 +144,60 @@ def tile_list_kvt_act_kernel(
             else:
                 nc.vector.tensor_scalar(out, bank[:], factor, None, MULT)
 
-        def keys(b, c, slot, on_vector=()):
-            rounded = ring.tile([P, 2048], BF16, name="rounded", tag="slot%d" % slot, align_bytes=64)
+        def keys(b, c, rounded, on_vector=()):
             for s in range(4):
                 bank = feature_product(wk_c, wk_s, b, lambda a: tab_operand(a, c, P * s, P))
                 relu_out("vector" if s in on_vector else "scalar", rounded[:, 512 * s : 512 * (s + 1)], bank)
-            return rounded
 
-        def quantize_keys(b, c, rounded):
-            quantize(ka_c[b], ka_s[b], CHUNK * c, CHUNK, rounded[:])
+        def key_scales(b, c):
+            n = 4 * b + c
+            if n == 0:
+                return ka_early_scales[:]
+            if n == 1:
+                return ka_middle_scales[:]
+            return ka_late_scales[:, CHUNK * (n - 2) : CHUNK * (n - 1)]
 
-        def queries(mt):
+        def quantize_keys(b, c):
+            nc.vector.quantize_mx(
+                out=ka_c[b][:, CHUNK * c : CHUNK * (c + 1)].bitcast(FP8X4), scales=key_scales(b, c), in_=key_rows[b, c][:]
+            )
+
+        def queries(mt, engines):
             for b in range(2):
-                rounded = ring.tile([P, 512], BF16, name="rounded_q", tag="rounded_q", bufs=3, align_bytes=64)
+                rounded = ring.tile([P, 512], BF16, name="rounded_q", tag="rounded_q", bufs=4, align_bytes=64)
                 bank = feature_product(
                     wq_c, wq_s, b, lambda a: (x_c[a][:, P * mt : P * (mt + 1)].bitcast(FP8X4), x_s[a][:, P * mt : P * (mt + 1)])
                 )
-                relu_out("vector" if mt < 1 or b == 1 else "scalar", rounded[:], bank)
+                relu_out(engines[b], rounded[:], bank)
                 quantize(qa_c[b], qa_s[b], P * mt, P, rounded[:])
 
-        def scores(mt, c, staged):
-            cols = slice(CHUNK * c, CHUNK * (c + 1))
-            bank = wide_product(qa_c, qa_s, P * mt, lambda b: (ka_c[b][:, cols].bitcast(FP8X4), ka_s[b][:, cols]))
-            scale_out("scalar" if (mt + c) % 2 == 0 else "vector", staged[:, cols], bank, SCORE_SCALE)
+        def scores(mt, c, engine, j0=0, width=CHUNK):
+            cols = slice(CHUNK * c + j0, CHUNK * c + j0 + width)
+            bank = wide_product(
+                qa_c, qa_s, P * mt, lambda b: (ka_c[b][:, cols].bitcast(FP8X4), key_scales(b, c)[:, j0 : j0 + width]), width
+            )
+            scale_out(engine, score_rows[mt][:, cols], bank, SCORE_SCALE)
 
+        def store_scores(mt, j0, j1):
+            nc.sync.dma_start(out_0[P * mt : P * (mt + 1), j0:j1], score_rows[mt][:, j0:j1])
+
+        def score_pair(mt, pair):
+            scores(mt, 2 * pair, "scalar")
+            scores(mt, 2 * pair + 1, "vector")
+            store_scores(mt, 1024 * pair, 1024 * (pair + 1))
 
         def values(nt, c):
             bank = wide_product(wv_c, wv_s, P * nt, lambda a: tab_operand(a, c, 0, CHUNK))
             nc.scalar.copy(value_rows[nt][:, CHUNK * c : CHUNK * (c + 1)], bank[:])
 
-        def wv_piece(a, c0, width, slot):
+        def wv_piece(a, c0, width):
             raw = wv_raw[a, c0 // 256][:, :, c0 % 256 : c0 % 256 + width]
-            quantize(wv_c[a], wv_s[a], c0, width, round_plain("scalar", raw, width, slot)[:])
+            quantize(wv_c[a], wv_s[a], c0, width, round_plain("scalar", raw, width, "wv%d_%d" % (a, c0))[:])
 
-        def feature_weights(codes, scales, raw, a, b, engine, slot):
-            quantize(codes[a], scales[a], 512 * b, 512, round_permuted(engine, raw, slot)[:])
+        def feature_weights(codes, scales, raw, a, b):
+            halves = [round_permuted(raw, half) for half in range(2)]
+            for half in range(2):
+                quantize(codes[a], scales[a], 512 * b + 256 * half, 256, halves[half][:])
 
         with tc.tile_pool(name="early", bufs=1) as early:
             table_scales = early.tile([P, T // 4], I32, name="table_scales")
@@ -204,91 +214,82 @@ def tile_list_kvt_act_kernel(
                 nc.sync.dma_start(table_scales[16 * g : 16 * (g + 1), :], rows[first : first + 16, :])
             nc.sync.dma_start(table_words[:], tab_words[0].rearrange("p t b -> p (t b)").bitcast(I32))
             wv_raw = {
-                (a, 0): load(ring.tile([P, 4, 256], F32, name="wv_low%d" % a)[:], wv, a, 0, 256) for a in range(2)
+                (a, 0): load(
+                    arena.tile([P, 4, 256], F32, name="wv_low%d" % a, offset=16384 + 4096 * a, align_bytes=64)[:], wv, a, 0, 256
+                )
+                for a in range(2)
             }
-            gather_scales(table_scales, 0)
-            gather_scales(table_scales, 1)
+            nc.vector.tensor_copy(picked_scales[:], table_scales[:].bitcast(U8).indirect(offsets[:]))
+            picked_rows = picked_scales[:].bitcast(I32)
+            nc.scalar.dma_start(second_scales[0:4, :], picked_rows[16:20, :])
+            nc.scalar.dma_start(second_scales[32:96, :], picked_rows[60:124, :])
+            nc.scalar.dma_start(second_scales[96:100, :], picked_rows[124:P, :])
 
         late = ctx.enter_context(tc.tile_pool(name="late", bufs=1))
         for a in range(2):
-            wv_raw[a, 1] = load(late.tile([P, 4, 256], F32, name="wv_high%d" % a)[:], wv, a, 256, 256)
+            wv_raw[a, 1] = load(
+                late.tile([P, 4, 256], F32, name="wv_high", tag="high%d" % a, align_bytes=64)[:], wv, a, 256, 256
+            )
         wk_raw = {}
         for b in range(2):
-            pair = late.tile([P, 2, 4, 512], F32, name="raw", tag="raw%d" % b)
             for a in range(2):
-                wk_raw[a, b] = load(pair[:, a], wk, a, 512 * b, 512)
+                wk_raw[a, b] = load(late.tile([P, 4, 512], F32, name="wk_raw", tag="wk%d" % (2 * b + a))[:], wk, a, 512 * b, 512)
+        wq_raw = [load(late.tile([P, 4, R], F32, name="wq_raw", tag="wq%d" % a, align_bytes=64)[:], wq, a, 0, R) for a in range(2)]
+        x_raw = [load(late.tile([P, 4, M], F32, name="x_raw", tag="x%d" % a, align_bytes=64)[:], x, a, 0, M) for a in range(2)]
 
-        part_words(0, gather_words(0, 0))
-        wv_piece(0, 0, 256, 4)
-        wv_piece(1, 0, 128, 5)
-        part_words(1, gather_words(1, 2))
-        wv_piece(1, 128, 128, 6)
-        part_words(2, gather_words(2, 5))
-        wv_piece(0, 256, 256, 4)
-        part_words(3, gather_words(3, 6))
-        wv_piece(1, 256, 256, 1)
+        picked = [gather_words(c, "cast") for c in range(2)]
+        part_words(0, picked[0])
+        wv_piece(0, 0, 256)
+        part_words(1, picked[1])
+        wv_piece(1, 0, 128)
+        wv_piece(1, 128, 128)
+        part_words(2, gather_words(2, "wv1_0"))
+        wv_piece(0, 256, 256)
+        wv_piece(1, 256, 128)
+        wv_piece(1, 384, 128)
+        part_words(3, gather_words(3, "wv1_256"))
 
-        value_rows = [ring.tile([P, J], F32, name="staged", tag="staged%d" % nt) for nt in range(4)]
-        for nt in range(4):
-            values(nt, 0)
-            values(nt, 1)
-        feature_weights(wk_c, wk_s, wk_raw[0, 0], 0, 0, "vector", 4)
-        feature_weights(wk_c, wk_s, wk_raw[1, 0], 1, 0, "vector", 4)
-        pair = late.tile([P, 2, 4, 512], F32, name="raw", tag="raw2")
-        x_raw = [load(pair[:, a], x, a, 0, M) for a in range(2)]
-        wq_raw = {}
-        for b, tag in enumerate(("raw3", "raw0")):
-            pair = late.tile([P, 2, 4, 512], F32, name="raw", tag=tag)
+        value_rows = [ring.tile([P, J], F32, name="value_rows%d" % nt) for nt in range(4)]
+        for pair, c in ((0, 0), (0, 1), (0, 2), (1, 0), (1, 1), (1, 2), (0, 3), (1, 3)):
+            values(2 * pair, c)
+            values(2 * pair + 1, c)
+        for b in range(2):
             for a in range(2):
-                wq_raw[a, b] = load(pair[:, a], wq, a, 512 * b, 512)
-        for c in (2, 3):
-            for nt in range(4):
-                values(nt, c)
-        feature_weights(wk_c, wk_s, wk_raw[0, 1], 0, 1, "vector", 4)
-        feature_weights(wk_c, wk_s, wk_raw[1, 1], 1, 1, "vector", 4)
+                feature_weights(wk_c, wk_s, wk_raw[a, b], a, b)
+        for a in range(2):
+            for b in range(2):
+                feature_weights(wq_c, wq_s, wq_raw[a][:, :, 512 * b : 512 * (b + 1)], a, b)
+        for a in range(2):
+            halves = [round_plain("vector", x_raw[a][:, :, 256 * h : 256 * (h + 1)], 256, "cast") for h in range(2)]
+            for h in range(2):
+                quantize(x_c[a], x_s[a], 256 * h, 256, halves[h][:])
         for nt in range(4):
             nc.sync.dma_start(out_1[P * nt : P * (nt + 1), :], value_rows[nt][:])
-        quantize_keys(0, 0, keys(0, 0, 0))
-        quantize(x_c[0], x_s[0], 0, M, round_plain("vector", x_raw[0], M, 4)[:])
-        quantize_keys(0, 1, keys(0, 1, 1))
-        quantize(x_c[1], x_s[1], 0, M, round_plain("vector", x_raw[1], M, 0)[:])
-        quantize_keys(0, 2, keys(0, 2, 2))
-        feature_weights(wq_c, wq_s, wq_raw[0, 0], 0, 0, "vector", 4)
-        quantize_keys(0, 3, keys(0, 3, 3))
-        feature_weights(wq_c, wq_s, wq_raw[1, 0], 1, 0, "vector", 0)
-        held = [keys(1, 0, 5)]
-        feature_weights(wq_c, wq_s, wq_raw[0, 1], 0, 1, "vector", 4)
-        quantize_keys(1, 0, held[0])
-        held.append(keys(1, 1, 6))
-        feature_weights(wq_c, wq_s, wq_raw[1, 1], 1, 1, "vector", 0)
-        quantize_keys(1, 1, held[1])
-        held.append(keys(1, 2, 7))
-        held.append(keys(1, 3, 8))
-        queries(0)
-        quantize_keys(1, 2, held[2])
-        quantize_keys(1, 3, held[3])
-        queries(1)
-        for mt in range(4):
-            if mt < 2:
-                queries(mt + 2)
-            staged = ring.tile([P, J], F32, name="staged", tag="staged%d" % mt)
-            out_rows = out_0[P * mt : P * (mt + 1), :]
-            if mt < 3:
-                for c in range(4):
-                    scores(mt, c, staged)
-                    if c % 2 == 1:
-                        cols = slice(CHUNK * (c - 1), CHUNK * (c + 1))
-                        nc.sync.dma_start(out_rows[:, cols], staged[:, cols])
+        key_rows = {}
+        for n in range(8):
+            if n < 6:
+                key_rows[n // 4, n % 4] = arena.tile([P, 2048], BF16, name="key_rows%d" % n, offset=4096 * n, align_bytes=64)
             else:
-                scores(mt, 0, staged)
-                scores(mt, 1, staged)
-                nc.sync.dma_start(out_rows[:, 0:1024], staged[:, 0:1024])
-                scores(mt, 2, staged)
-                nc.sync.dma_start(out_rows[:, 1024:1536], staged[:, 1024:1536])
-                for half, engine in enumerate(("vector", "scalar")):
-                    cols = slice(J - 512 + 256 * half, J - 256 + 256 * half)
-                    bank = wide_product(
-                        qa_c, qa_s, P * mt, lambda b: (ka_c[b][:, cols].bitcast(FP8X4), ka_s[b][:, cols]), 256
-                    )
-                    scale_out(engine, staged[:, cols], bank, SCORE_SCALE)
-                    nc.sync.dma_start(out_rows[:, cols], staged[:, cols])
+                key_rows[n // 4, n % 4] = late.tile([P, 2048], BF16, name="key_rows", tag="high%d" % (n - 6), align_bytes=64)
+        ka_late_scales = late.tile([P, 6 * CHUNK], U8, name="ka_late_scales", tag="x1", align_bytes=64)
+        ka_middle_scales = late.tile([P, CHUNK], U8, name="ka_middle_scales", tag="wq0", align_bytes=64)
+        score_rows = [late.tile([P, J], F32, name="score_rows", tag="wk%d" % mt) for mt in range(4)]
+        for n in range(8):
+            keys(n // 4, n % 4, key_rows[n // 4, n % 4])
+        for b, c in ((0, 0), (0, 1), (1, 0), (1, 1), (0, 2), (0, 3)):
+            quantize_keys(b, c)
+        queries(0, ("vector", "vector"))
+        quantize_keys(1, 2)
+        quantize_keys(1, 3)
+        queries(1, ("scalar", "scalar"))
+        for mt in range(3):
+            score_pair(mt, 0)
+            if mt < 2:
+                queries(mt + 2, ("scalar", "vector"))
+            score_pair(mt, 1)
+        score_pair(3, 0)
+        scores(3, 2, "scalar")
+        store_scores(3, 1024, 1536)
+        for half, engine in enumerate(("vector", "scalar")):
+            scores(3, 3, engine, 256 * half, 256)
+            store_scores(3, 1536 + 256 * half, 1792 + 256 * half)

@@ -21,6 +21,11 @@ MULT = mybir.AluOpType.mult
 P = 128
 PASS = 512
 CHUNK = 512
+HALF = 256
+BANKS = 8
+CAST_BUFS = 4
+KEY_ROW_BYTES = 8 * CHUNK
+ARENA_KEY_ROWS = 6
 SCORE_SCALE = 0.03125
 
 
@@ -31,14 +36,19 @@ def tile_list_kvt_act_kernel(
     with ExitStack() as ctx:
         keep = ctx.enter_context(tc.tile_pool(name="keep", bufs=1))
         ring = ctx.enter_context(tc.tile_pool(name="ring", bufs=1))
-        psum = ctx.enter_context(tc.psum_pool(name="psum", bufs=8))
+        psum = ctx.enter_context(tc.psum_pool(name="psum", bufs=1))
+        banks_taken = []
+
+        def new_bank(width):
+            banks_taken.append(len(banks_taken) % BANKS)
+            return psum.tile([P, width], F32, name="bank", tag="bank%d" % banks_taken[-1])
 
         offsets = keep.tile([P, J // 16], U16, name="offsets")
         arena = ctx.enter_context(tc.tile_pool(name="arena", bufs=1))
         table_words = arena.tile([P, T], I32, name="table_words", offset=0, align_bytes=64)
         picked_scales = keep.tile([P, J], U8, name="picked_scales", align_bytes=64)
         second_scales = keep.tile([P, J // 4], I32, name="second_scales", align_bytes=64)
-        tab_codes = [keep.tile([P, 2, CHUNK], U16, name="tab_codes%d" % c, align_bytes=64) for c in range(4)]
+        tab_codes = {}
 
         def codes_pair(name, width):
             return (
@@ -52,14 +62,13 @@ def tile_list_kvt_act_kernel(
         x_c, x_s = codes_pair("x", M)
         qa_c, qa_s = codes_pair("qa", M)
         ka_c = [keep.tile([P, J], U32, name="ka_codes%d" % b, align_bytes=64) for b in range(2)]
-        ka_early_scales = keep.tile([P, CHUNK], U8, name="ka_early_scales", align_bytes=64)
 
         def load(raw, w, a, c0, width):
             nc.sync.dma_start(raw, w[PASS * a : PASS * (a + 1), c0 : c0 + width].rearrange("(p j) c -> p j c", j=4))
             return raw
 
         def staging(dtype, width, tag):
-            bufs = 4 if tag == "cast" else 1
+            bufs = CAST_BUFS if tag == "cast" else 1
             return ring.tile([P, width], dtype, name="staging", tag=tag, bufs=bufs, align_bytes=64)
 
         def round_plain(engine, raw, width, tag):
@@ -72,11 +81,11 @@ def tile_list_kvt_act_kernel(
                 nc.vector.tensor_copy(out, in_)
             return grouped
 
-        def round_permuted(raw, half):
-            grouped = staging(BF16, 1024, "cast")
+        def round_permuted(raw, h, tag):
+            grouped = staging(BF16, 4 * HALF, tag)
             nc.vector.tensor_copy(
                 grouped[:].rearrange("p (t c i j) -> p t c j i", t=2, i=4, j=4),
-                raw.rearrange("p j (c t i) -> p t c j i", t=4, i=4)[:, 2 * half : 2 * half + 2],
+                raw.rearrange("p j (c t i) -> p t c j i", t=4, i=4)[:, 2 * h : 2 * h + 2],
             )
             return grouped
 
@@ -85,25 +94,24 @@ def tile_list_kvt_act_kernel(
                 out=codes[:, c0 : c0 + width].bitcast(FP8X4), scales=scales[:, c0 : c0 + width], in_=grouped
             )
 
-        def gather_words(c, tag):
-            picked = staging(U32, CHUNK, tag)
+        def gather_words(c, picked):
             nc.vector.tensor_copy(picked[:], table_words[:].bitcast(U32).indirect(offsets[:, 32 * c : 32 * (c + 1)]))
             return picked
 
-        def part_words(c, picked):
+        def part_words(c, picked, tag):
+            tab_codes[c] = ring.tile([P, 2, CHUNK], U16, name="tab_codes", tag=tag, bufs=1, align_bytes=64)
             nc.vector.tensor_copy(tab_codes[c][:], picked[:].bitcast(U16).rearrange("p (j d) -> p d j", d=2))
 
         def tab_operand(a, c, j0, width):
             codes = tab_codes[c][:, a, j0 : j0 + width].bitcast(U8).bitcast(FP4X4)
-            plane = picked_scales[:] if a == 0 else second_scales[:].bitcast(U8)
-            return codes, plane[:, CHUNK * c + j0 : CHUNK * c + j0 + width]
+            scale_rows = picked_scales[:] if a == 0 else second_scales[:].bitcast(U8)
+            return codes, scale_rows[:, CHUNK * c + j0 : CHUNK * c + j0 + width]
 
-        def wide_product(lhs_c, lhs_s, m0, rhs_of_pass, width=512):
-            bank = psum.tile([P, width], F32, name="bank", tag="bank")
+        def two_passes(out, lhs_c, lhs_s, m0, rhs_of_pass):
             for a in range(2):
                 codes, scales = rhs_of_pass(a)
                 nc.tensor.matmul_mx(
-                    out=bank[:],
+                    out=out,
                     lhsT=lhs_c[a][:, m0 : m0 + P].bitcast(FP8X4),
                     lhsT_scale=lhs_s[a][:, m0 : m0 + P],
                     rhs=codes,
@@ -111,93 +119,65 @@ def tile_list_kvt_act_kernel(
                     start=(a == 0),
                     stop=(a == 1),
                 )
-            return bank
 
-        def feature_product(w_c, w_s, b, rhs_of_pass):
-            bank = psum.tile([P, 512], F32, name="bank", tag="bank")
+        def features(w_c, w_s, b, rhs_of_pass, engine, rows):
+            bank = new_bank(CHUNK)
             for t in range(4):
-                m0 = PASS * b + P * t
-                for a in range(2):
-                    codes, scales = rhs_of_pass(a)
-                    nc.tensor.matmul_mx(
-                        out=bank[:, P * t : P * (t + 1)],
-                        lhsT=w_c[a][:, m0 : m0 + P].bitcast(FP8X4),
-                        lhsT_scale=w_s[a][:, m0 : m0 + P],
-                        rhs=codes,
-                        rhs_scale=scales,
-                        start=(a == 0),
-                        stop=(a == 1),
-                    )
-            return bank
-
-        def relu_out(engine, out, bank):
-            view_out = out.rearrange("p (j t) -> p j t", t=4)
-            view_in = bank[:].rearrange("p (t j) -> p j t", t=4)
+                two_passes(bank[:, P * t : P * (t + 1)], w_c, w_s, PASS * b + P * t, rhs_of_pass)
+            view_out = rows.rearrange("p (j i t) -> p j t i", t=4, i=2)
+            view_in = bank[:].rearrange("p (t j i) -> p j t i", t=4, i=2)
             if engine == "scalar":
                 nc.scalar.activation(view_out, view_in, RELU)
             else:
                 nc.vector.tensor_scalar(view_out, view_in, 0.0, None, MAX)
 
-        def scale_out(engine, out, bank, factor):
-            if engine == "scalar":
-                nc.scalar.activation(out, bank[:], COPY, scale=factor)
-            else:
-                nc.vector.tensor_scalar(out, bank[:], factor, None, MULT)
-
-        def keys(b, c, rounded, on_vector=()):
-            for s in range(4):
-                bank = feature_product(wk_c, wk_s, b, lambda a: tab_operand(a, c, P * s, P))
-                relu_out("vector" if s in on_vector else "scalar", rounded[:, 512 * s : 512 * (s + 1)], bank)
-
-        def key_scales(b, c):
-            n = 4 * b + c
-            if n == 0:
-                return ka_early_scales[:]
-            if n == 1:
-                return ka_middle_scales[:]
-            return ka_late_scales[:, CHUNK * (n - 2) : CHUNK * (n - 1)]
-
-        def quantize_keys(b, c):
-            nc.vector.quantize_mx(
-                out=ka_c[b][:, CHUNK * c : CHUNK * (c + 1)].bitcast(FP8X4), scales=key_scales(b, c), in_=key_rows[b, c][:]
-            )
-
-        def queries(mt, engines):
-            for b in range(2):
-                rounded = ring.tile([P, 512], BF16, name="rounded_q", tag="rounded_q", bufs=4, align_bytes=64)
-                bank = feature_product(
-                    wq_c, wq_s, b, lambda a: (x_c[a][:, P * mt : P * (mt + 1)].bitcast(FP8X4), x_s[a][:, P * mt : P * (mt + 1)])
-                )
-                relu_out(engines[b], rounded[:], bank)
-                quantize(qa_c[b], qa_s[b], P * mt, P, rounded[:])
-
-        def scores(mt, c, engine, j0=0, width=CHUNK):
-            cols = slice(CHUNK * c + j0, CHUNK * c + j0 + width)
-            bank = wide_product(
-                qa_c, qa_s, P * mt, lambda b: (ka_c[b][:, cols].bitcast(FP8X4), key_scales(b, c)[:, j0 : j0 + width]), width
-            )
-            scale_out(engine, score_rows[mt][:, cols], bank, SCORE_SCALE)
-
-        def store_scores(mt, j0, j1):
-            nc.sync.dma_start(out_0[P * mt : P * (mt + 1), j0:j1], score_rows[mt][:, j0:j1])
-
-        def score_pair(mt, pair):
-            scores(mt, 2 * pair, "scalar")
-            scores(mt, 2 * pair + 1, "vector")
-            store_scores(mt, 1024 * pair, 1024 * (pair + 1))
-
         def values(nt, c):
-            bank = wide_product(wv_c, wv_s, P * nt, lambda a: tab_operand(a, c, 0, CHUNK))
+            bank = new_bank(CHUNK)
+            two_passes(bank[:], wv_c, wv_s, P * nt, lambda a: tab_operand(a, c, 0, CHUNK))
             nc.scalar.copy(value_rows[nt][:, CHUNK * c : CHUNK * (c + 1)], bank[:])
 
+        def keys(b, c):
+            for s in range(4):
+                rows = key_rows[b, c][:, 4 * P * s : 4 * P * (s + 1)]
+                features(wk_c, wk_s, b, lambda a: tab_operand(a, c, P * s, P), "scalar", rows)
+
+        def quantize_keys(b, c):
+            quantize(ka_c[b], ka_s[b], CHUNK * c, CHUNK, key_rows[b, c][:])
+
+        def queries(b, mt, engine):
+            cols = slice(P * mt, P * (mt + 1))
+            rows = query_rows[:, b, 4 * P * mt : 4 * P * (mt + 1)]
+            features(wq_c, wq_s, b, lambda a: (x_c[a][:, cols].bitcast(FP8X4), x_s[a][:, cols]), engine, rows)
+
+        def quantize_queries(b, mt, count):
+            quantize(qa_c[b], qa_s[b], P * mt, P * count, query_rows[:, b, 4 * P * mt : 4 * P * (mt + count)])
+
+        def scores(mt, j0, width, engine):
+            cols = slice(j0, j0 + width)
+            bank = new_bank(width)
+            two_passes(bank[:], qa_c, qa_s, P * mt, lambda b: (ka_c[b][:, cols].bitcast(FP8X4), ka_s[b][:, cols]))
+            if engine == "scalar":
+                nc.scalar.activation(score_rows[mt][:, cols], bank[:], COPY, scale=SCORE_SCALE)
+            else:
+                nc.vector.tensor_scalar(score_rows[mt][:, cols], bank[:], SCORE_SCALE, None, MULT)
+
+        def store_scores(mt, j0, width):
+            nc.sync.dma_start(out_0[P * mt : P * (mt + 1), j0 : j0 + width], score_rows[mt][:, j0 : j0 + width])
+
+        def score_pair(mt, pair, second):
+            j0 = 2 * CHUNK * pair
+            scores(mt, j0, CHUNK, "scalar")
+            scores(mt, j0 + CHUNK, CHUNK, second)
+            store_scores(mt, j0, 2 * CHUNK)
+
         def wv_piece(a, c0, width):
-            raw = wv_raw[a, c0 // 256][:, :, c0 % 256 : c0 % 256 + width]
+            raw = wv_raw[a, c0 // HALF][:, :, c0 % HALF : c0 % HALF + width]
             quantize(wv_c[a], wv_s[a], c0, width, round_plain("scalar", raw, width, "wv%d_%d" % (a, c0))[:])
 
-        def feature_weights(codes, scales, raw, a, b):
-            halves = [round_permuted(raw, half) for half in range(2)]
-            for half in range(2):
-                quantize(codes[a], scales[a], 512 * b + 256 * half, 256, halves[half][:])
+        def feature_weights(codes, scales, raw, a, b, tags=("cast", "cast")):
+            halves = [round_permuted(raw, h, tags[h]) for h in range(2)]
+            for h in range(2):
+                quantize(codes[a], scales[a], PASS * b + HALF * h, HALF, halves[h][:])
 
         with tc.tile_pool(name="early", bufs=1) as early:
             table_scales = early.tile([P, T // 4], I32, name="table_scales")
@@ -207,89 +187,114 @@ def tile_list_kvt_act_kernel(
             nc.vector.memset(warm_in[:], 0.0)
             nc.scalar.activation(warm_out[:], warm_in[:], RELU)
             nc.sync.dma_start(offsets[:], offs)
-            rows = tab_scales.rearrange("a q t -> (a q) t").bitcast(I32)
-            nc.sync.dma_start(table_scales[0:32, :], rows)
+            scale_rows_hbm = tab_scales.rearrange("a q t -> (a q) t").bitcast(I32)
+            nc.sync.dma_start(table_scales[0:32, :], scale_rows_hbm)
             for g in range(2, 8):
                 first = 4 * (g // 2) + 4 * (g % 2)
-                nc.sync.dma_start(table_scales[16 * g : 16 * (g + 1), :], rows[first : first + 16, :])
+                nc.sync.dma_start(table_scales[16 * g : 16 * (g + 1), :], scale_rows_hbm[first : first + 16, :])
             nc.sync.dma_start(table_words[:], tab_words[0].rearrange("p t b -> p (t b)").bitcast(I32))
-            wv_raw = {
-                (a, 0): load(
-                    arena.tile([P, 4, 256], F32, name="wv_low%d" % a, offset=16384 + 4096 * a, align_bytes=64)[:], wv, a, 0, 256
-                )
-                for a in range(2)
-            }
+            wv_raw = {}
+            for a in range(2):
+                low = arena.tile([P, 4, HALF], F32, name="wv_low%d" % a, offset=4 * T + 16 * HALF * a, align_bytes=64)
+                wv_raw[a, 0] = load(low[:], wv, a, 0, HALF)
             nc.vector.tensor_copy(picked_scales[:], table_scales[:].bitcast(U8).indirect(offsets[:]))
             picked_rows = picked_scales[:].bitcast(I32)
-            nc.scalar.dma_start(second_scales[0:4, :], picked_rows[16:20, :])
-            nc.scalar.dma_start(second_scales[32:96, :], picked_rows[60:124, :])
-            nc.scalar.dma_start(second_scales[96:100, :], picked_rows[124:P, :])
+            nc.sync.dma_start(second_scales[0:4, :], picked_rows[16:20, :])
+            nc.sync.dma_start(second_scales[32:96, :], picked_rows[60:124, :])
+            nc.sync.dma_start(second_scales[96:100, :], picked_rows[124:P, :])
 
         late = ctx.enter_context(tc.tile_pool(name="late", bufs=1))
+        wv_high = late.tile([P, 2, 4, HALF], F32, name="wv_high", tag="high", align_bytes=64)
         for a in range(2):
-            wv_raw[a, 1] = load(
-                late.tile([P, 4, 256], F32, name="wv_high", tag="high%d" % a, align_bytes=64)[:], wv, a, 256, 256
-            )
+            wv_raw[a, 1] = load(wv_high[:, a], wv, a, HALF, HALF)
         wk_raw = {}
         for b in range(2):
             for a in range(2):
-                wk_raw[a, b] = load(late.tile([P, 4, 512], F32, name="wk_raw", tag="wk%d" % (2 * b + a))[:], wk, a, 512 * b, 512)
-        wq_raw = [load(late.tile([P, 4, R], F32, name="wq_raw", tag="wq%d" % a, align_bytes=64)[:], wq, a, 0, R) for a in range(2)]
-        x_raw = [load(late.tile([P, 4, M], F32, name="x_raw", tag="x%d" % a, align_bytes=64)[:], x, a, 0, M) for a in range(2)]
+                raw = late.tile([P, 4, PASS], F32, name="wk_raw", tag="wk%d" % (2 * b + a), align_bytes=64)
+                wk_raw[a, b] = load(raw[:], wk, a, PASS * b, PASS)
+        wq_first = load(late.tile([P, 4, R], F32, name="wq_first")[:], wq, 0, 0, R)
+        x_raw = [
+            load(late.tile([P, 4, M], F32, name="x_raw", tag="x%d" % a, align_bytes=64)[:], x, a, 0, M) for a in range(2)
+        ]
+        wq_second = [
+            load(late.tile([P, 4, PASS], F32, name="wq_second", tag="wq%d" % b, align_bytes=64)[:], wq, 1, PASS * b, PASS)
+            for b in range(2)
+        ]
 
-        picked = [gather_words(c, "cast") for c in range(2)]
-        part_words(0, picked[0])
-        wv_piece(0, 0, 256)
-        part_words(1, picked[1])
-        wv_piece(1, 0, 128)
-        wv_piece(1, 128, 128)
-        part_words(2, gather_words(2, "wv1_0"))
-        wv_piece(0, 256, 256)
-        wv_piece(1, 256, 128)
-        wv_piece(1, 384, 128)
-        part_words(3, gather_words(3, "wv1_256"))
+        picked = [gather_words(c, staging(U32, CHUNK, "cast")) for c in range(2)]
+        part_words(0, picked[0], "tab0")
+        wv_piece(0, 0, P)
+        wv_piece(1, 0, P)
+        part_words(1, picked[1], "wv0_0")
+        wv_piece(0, P, P)
+        wv_piece(1, P, P)
+        part_words(2, gather_words(2, staging(U32, CHUNK, "wv1_0")), "tab2")
+        wv_piece(0, HALF, HALF)
+        wv_piece(1, HALF, P)
+        wv_piece(1, HALF + P, P)
+        part_words(3, gather_words(3, staging(U32, CHUNK, "wv1_256")), "tab3")
 
-        value_rows = [ring.tile([P, J], F32, name="value_rows%d" % nt) for nt in range(4)]
-        for pair, c in ((0, 0), (0, 1), (0, 2), (1, 0), (1, 1), (1, 2), (0, 3), (1, 3)):
-            values(2 * pair, c)
-            values(2 * pair + 1, c)
+        first_rows = late.tile([P, 2, J], F32, name="first_rows", tag="high", align_bytes=64)
+        value_rows = [first_rows[:, nt] for nt in range(2)]
+        value_rows.extend(ring.tile([P, J], F32, name="value_rows%d" % nt)[:] for nt in (2, 3))
+        for chunks in ((0, 1, 2), (3,)):
+            for first_tile in (0, 2):
+                for c in chunks:
+                    values(first_tile, c)
+                    values(first_tile + 1, c)
+
+        feature_weights(wk_c, wk_s, wk_raw[0, 0], 0, 0, ("wv1_384", "wv1_256"))
+        feature_weights(wk_c, wk_s, wk_raw[1, 0], 1, 0)
+        for a in range(2):
+            feature_weights(wk_c, wk_s, wk_raw[a, 1], a, 1)
         for b in range(2):
-            for a in range(2):
-                feature_weights(wk_c, wk_s, wk_raw[a, b], a, b)
+            feature_weights(wq_c, wq_s, wq_first[:, :, PASS * b : PASS * (b + 1)], 0, b)
         for a in range(2):
-            for b in range(2):
-                feature_weights(wq_c, wq_s, wq_raw[a][:, :, 512 * b : 512 * (b + 1)], a, b)
-        for a in range(2):
-            halves = [round_plain("vector", x_raw[a][:, :, 256 * h : 256 * (h + 1)], 256, "cast") for h in range(2)]
+            halves = [round_plain("vector", x_raw[a][:, :, HALF * h : HALF * (h + 1)], HALF, "cast") for h in range(2)]
             for h in range(2):
-                quantize(x_c[a], x_s[a], 256 * h, 256, halves[h][:])
+                quantize(x_c[a], x_s[a], HALF * h, HALF, halves[h][:])
+        for b in range(2):
+            feature_weights(wq_c, wq_s, wq_second[b], 1, b)
         for nt in range(4):
-            nc.sync.dma_start(out_1[P * nt : P * (nt + 1), :], value_rows[nt][:])
+            nc.sync.dma_start(out_1[P * nt : P * (nt + 1), :], value_rows[nt])
+
         key_rows = {}
         for n in range(8):
-            if n < 6:
-                key_rows[n // 4, n % 4] = arena.tile([P, 2048], BF16, name="key_rows%d" % n, offset=4096 * n, align_bytes=64)
+            if n < ARENA_KEY_ROWS:
+                rows = arena.tile([P, 4 * CHUNK], BF16, name="key_rows%d" % n, offset=KEY_ROW_BYTES * n, align_bytes=64)
             else:
-                key_rows[n // 4, n % 4] = late.tile([P, 2048], BF16, name="key_rows", tag="high%d" % (n - 6), align_bytes=64)
-        ka_late_scales = late.tile([P, 6 * CHUNK], U8, name="ka_late_scales", tag="x1", align_bytes=64)
-        ka_middle_scales = late.tile([P, CHUNK], U8, name="ka_middle_scales", tag="wq0", align_bytes=64)
-        score_rows = [late.tile([P, J], F32, name="score_rows", tag="wk%d" % mt) for mt in range(4)]
-        for n in range(8):
-            keys(n // 4, n % 4, key_rows[n // 4, n % 4])
-        for b, c in ((0, 0), (0, 1), (1, 0), (1, 1), (0, 2), (0, 3)):
-            quantize_keys(b, c)
-        queries(0, ("vector", "vector"))
-        quantize_keys(1, 2)
-        quantize_keys(1, 3)
-        queries(1, ("scalar", "scalar"))
+                rows = ring.tile([P, 4 * CHUNK], BF16, name="key_rows%d" % n, align_bytes=64)
+            key_rows[divmod(n, 4)] = rows
+        ka_scale_rows = late.tile([P, 2 * J], U8, name="ka_scales", tag="wq1", align_bytes=64)
+        ka_s = [ka_scale_rows[:, J * b : J * (b + 1)] for b in range(2)]
+        score_rows = [late.tile([P, J], F32, name="score_rows", tag="wk%d" % mt, align_bytes=64) for mt in range(4)]
+        query_rows = late.tile([P, 2, 4 * M], BF16, name="query_rows", tag="x1", align_bytes=64)
+
+        for n in range(7):
+            keys(*divmod(n, 4))
+        for mt in range(4):
+            queries(0, mt, "scalar")
+        keys(1, 3)
+        for c in range(2):
+            for b in range(2):
+                quantize_keys(b, c)
+        quantize_queries(0, 0, 4)
         for mt in range(3):
-            score_pair(mt, 0)
-            if mt < 2:
-                queries(mt + 2, ("scalar", "vector"))
-            score_pair(mt, 1)
-        score_pair(3, 0)
-        scores(3, 2, "scalar")
-        store_scores(3, 1024, 1536)
-        for half, engine in enumerate(("vector", "scalar")):
-            scores(3, 3, engine, 256 * half, 256)
-            store_scores(3, 1536 + 256 * half, 1792 + 256 * half)
+            queries(1, mt, ("vector", "scalar")[mt % 2])
+            quantize_queries(1, mt, 1)
+        score_pair(0, 0, "scalar")
+        queries(1, 3, "vector")
+        quantize_queries(1, 3, 1)
+        for c in (2, 3):
+            for b in range(2):
+                quantize_keys(b, c)
+        score_pair(1, 0, "scalar")
+        score_pair(2, 0, "vector")
+        score_pair(3, 0, "vector")
+        for mt in range(3):
+            score_pair(mt, 1, "vector")
+        scores(3, 2 * CHUNK, CHUNK, "scalar")
+        store_scores(3, 2 * CHUNK, CHUNK)
+        for h, engine in enumerate(("vector", "scalar")):
+            scores(3, 3 * CHUNK + HALF * h, HALF, engine)
+            store_scores(3, 3 * CHUNK + HALF * h, HALF)

@@ -188,25 +188,23 @@ def tile_list_kvt_act_kernel(
             nc.scalar.activation(warm_out[:], warm_in[:], RELU)
             nc.sync.dma_start(offsets[:], offs)
             scale_rows_hbm = tab_scales.rearrange("a q t -> (a q) t").bitcast(I32)
-            nc.sync.dma_start(table_scales[0:32, :], scale_rows_hbm)
-            for g in range(2, 8):
-                first = 4 * (g // 2) + 4 * (g % 2)
-                nc.sync.dma_start(table_scales[16 * g : 16 * (g + 1), :], scale_rows_hbm[first : first + 16, :])
+            nc.sync.dma_start(table_scales[0:P:4, :], tab_scales.rearrange("a q t -> q a t").bitcast(I32))
+            for i in range(1, 4):
+                rows = scale_rows_hbm[i : i + 16, :].unsqueeze(1).broadcast_to([16, 2, T // 4])
+                nc.sync.dma_start(table_scales[i:P:4, :], rows)
             nc.sync.dma_start(table_words[:], tab_words[0].rearrange("p t b -> p (t b)").bitcast(I32))
             wv_raw = {}
             for a in range(2):
                 low = arena.tile([P, 4, HALF], F32, name="wv_low%d" % a, offset=4 * T + 16 * HALF * a, align_bytes=64)
                 wv_raw[a, 0] = load(low[:], wv, a, 0, HALF)
+            wv_raw[0, 1] = load(ring.tile([P, 4, HALF], F32, name="wv_high0", align_bytes=64)[:], wv, 0, HALF, HALF)
             nc.vector.tensor_copy(picked_scales[:], table_scales[:].bitcast(U8).indirect(offsets[:]))
             picked_rows = picked_scales[:].bitcast(I32)
-            nc.sync.dma_start(second_scales[0:4, :], picked_rows[16:20, :])
-            nc.sync.dma_start(second_scales[32:96, :], picked_rows[60:124, :])
-            nc.sync.dma_start(second_scales[96:100, :], picked_rows[124:P, :])
+            for q in range(4):
+                nc.sync.dma_start(second_scales[32 * q : 32 * q + 4, :], picked_rows[32 * q + 4 : 32 * q + 32 : 8, :])
 
         late = ctx.enter_context(tc.tile_pool(name="late", bufs=1))
-        wv_high = late.tile([P, 2, 4, HALF], F32, name="wv_high", tag="high", align_bytes=64)
-        for a in range(2):
-            wv_raw[a, 1] = load(wv_high[:, a], wv, a, HALF, HALF)
+        wv_raw[1, 1] = load(late.tile([P, 4, HALF], F32, name="wv_high1", tag="high", align_bytes=64)[:], wv, 1, HALF, HALF)
         wk_raw = {}
         for b in range(2):
             for a in range(2):
@@ -221,29 +219,29 @@ def tile_list_kvt_act_kernel(
             for b in range(2)
         ]
 
-        picked = [gather_words(c, staging(U32, CHUNK, "cast")) for c in range(2)]
-        part_words(0, picked[0], "tab0")
-        wv_piece(0, 0, P)
+        part_words(0, gather_words(0, staging(U32, CHUNK, "cast")), "tab0")
+        wv_piece(0, 0, HALF)
         wv_piece(1, 0, P)
-        part_words(1, picked[1], "wv0_0")
-        wv_piece(0, P, P)
+        picked = gather_words(1, staging(U32, CHUNK, "wv1_0"))
         wv_piece(1, P, P)
-        part_words(2, gather_words(2, staging(U32, CHUNK, "wv1_0")), "tab2")
+        part_words(1, picked, "wv1_128")
         wv_piece(0, HALF, HALF)
+        picked = gather_words(2, staging(U32, CHUNK, "wv0_256"))
         wv_piece(1, HALF, P)
         wv_piece(1, HALF + P, P)
-        part_words(3, gather_words(3, staging(U32, CHUNK, "wv1_256")), "tab3")
+        part_words(2, picked, "wv1_256")
+        part_words(3, gather_words(3, staging(U32, CHUNK, "wv1_384")), "tab3")
 
         first_rows = late.tile([P, 2, J], F32, name="first_rows", tag="high", align_bytes=64)
         value_rows = [first_rows[:, nt] for nt in range(2)]
         value_rows.extend(ring.tile([P, J], F32, name="value_rows%d" % nt)[:] for nt in (2, 3))
-        for chunks in ((0, 1, 2), (3,)):
+        for chunks in ((0, 1), (2,), (3,)):
             for first_tile in (0, 2):
                 for c in chunks:
                     values(first_tile, c)
                     values(first_tile + 1, c)
 
-        feature_weights(wk_c, wk_s, wk_raw[0, 0], 0, 0, ("wv1_384", "wv1_256"))
+        feature_weights(wk_c, wk_s, wk_raw[0, 0], 0, 0, ("wv1_384", "cast"))
         feature_weights(wk_c, wk_s, wk_raw[1, 0], 1, 0)
         for a in range(2):
             feature_weights(wk_c, wk_s, wk_raw[a, 1], a, 1)
@@ -265,15 +263,15 @@ def tile_list_kvt_act_kernel(
             else:
                 rows = ring.tile([P, 4 * CHUNK], BF16, name="key_rows%d" % n, align_bytes=64)
             key_rows[divmod(n, 4)] = rows
-        ka_scale_rows = late.tile([P, 2 * J], U8, name="ka_scales", tag="wq1", align_bytes=64)
+        ka_scale_rows = late.tile([P, 2 * J], U8, name="ka_scales", tag="wq0", align_bytes=64)
         ka_s = [ka_scale_rows[:, J * b : J * (b + 1)] for b in range(2)]
         score_rows = [late.tile([P, J], F32, name="score_rows", tag="wk%d" % mt, align_bytes=64) for mt in range(4)]
-        query_rows = late.tile([P, 2, 4 * M], BF16, name="query_rows", tag="x1", align_bytes=64)
+        query_rows = late.tile([P, 2, 4 * M], BF16, name="query_rows", tag="wq1", align_bytes=64)
 
         for n in range(7):
             keys(*divmod(n, 4))
         for mt in range(4):
-            queries(0, mt, "scalar")
+            queries(0, mt, "vector")
         keys(1, 3)
         for c in range(2):
             for b in range(2):

@@ -46,22 +46,30 @@ def tile_list_kvt_act_kernel(
         offsets = keep.tile([P, J // 16], U16, name="offsets")
         arena = ctx.enter_context(tc.tile_pool(name="arena", bufs=1))
         table_words = arena.tile([P, T], I32, name="table_words", offset=0, align_bytes=64)
-        picked_scales = keep.tile([P, J], U8, name="picked_scales", align_bytes=64)
-        second_scales = keep.tile([P, J // 4], I32, name="second_scales", align_bytes=64)
+        operands = ctx.enter_context(tc.tile_pool(name="operands", bufs=1))
+        ends = [0]
+
+        def operand(name, dtype, width, size, start):
+            offset = (ends[-1] - start + 255) // 256 * 256 + start
+            ends.append(offset + width * size)
+            return operands.tile([P, width], dtype, name=name, offset=offset, align_bytes=64 if start else 256)
+
         tab_codes = {}
 
-        def codes_pair(name, width):
+        def codes_pair(name, width, code_start, scale_start):
             return (
-                [keep.tile([P, width], U32, name="%s_codes%d" % (name, a), align_bytes=64) for a in range(2)],
-                [keep.tile([P, width], U8, name="%s_scales%d" % (name, a), align_bytes=64) for a in range(2)],
+                [operand("%s_codes%d" % (name, a), U32, width, 4, code_start) for a in range(2)],
+                [operand("%s_scales%d" % (name, a), U8, width, 1, scale_start) for a in range(2)],
             )
 
-        wv_c, wv_s = codes_pair("wv", N)
-        wk_c, wk_s = codes_pair("wk", R)
-        wq_c, wq_s = codes_pair("wq", R)
-        x_c, x_s = codes_pair("x", M)
-        qa_c, qa_s = codes_pair("qa", M)
-        ka_c = [keep.tile([P, J], U32, name="ka_codes%d" % b, align_bytes=64) for b in range(2)]
+        wv_c, wv_s = codes_pair("wv", N, 0, 64)
+        wk_c, wk_s = codes_pair("wk", R, 0, 64)
+        wq_c, wq_s = codes_pair("wq", R, 0, 64)
+        x_c, x_s = codes_pair("x", M, 128, 192)
+        qa_c, qa_s = codes_pair("qa", M, 0, 64)
+        ka_c = [operand("ka_codes%d" % b, U32, J, 4, 128) for b in range(2)]
+        picked_scales = operand("picked_scales", U8, J, 1, 192)
+        second_scales = operand("second_scales", I32, J // 4, 4, 192)
 
         def load(raw, w, a, c0, width):
             nc.sync.dma_start(raw, w[PASS * a : PASS * (a + 1), c0 : c0 + width].rearrange("(p j) c -> p j c", j=4))
@@ -69,7 +77,7 @@ def tile_list_kvt_act_kernel(
 
         def staging(dtype, width, tag):
             bufs = CAST_BUFS if tag == "cast" else 1
-            return ring.tile([P, width], dtype, name="staging", tag=tag, bufs=bufs, align_bytes=64)
+            return ring.tile([P, width], dtype, name="staging", tag=tag, bufs=bufs, align_bytes=256)
 
         def round_plain(engine, raw, width, tag):
             grouped = staging(BF16, 4 * width, tag)
@@ -99,11 +107,12 @@ def tile_list_kvt_act_kernel(
             return picked
 
         def part_words(c, picked, tag):
-            tab_codes[c] = ring.tile([P, 2, CHUNK], U16, name="tab_codes", tag=tag, bufs=1, align_bytes=64)
-            nc.vector.tensor_copy(tab_codes[c][:], picked[:].bitcast(U16).rearrange("p (j d) -> p d j", d=2))
+            padded = ring.tile([P, 2 * CHUNK + 64], U16, name="tab_codes", tag=tag, bufs=1, align_bytes=256)
+            tab_codes[c] = padded[:, 64:]
+            nc.vector.tensor_copy(tab_codes[c].rearrange("p (d j) -> p d j", d=2), picked[:].bitcast(U16).rearrange("p (j d) -> p d j", d=2))
 
         def tab_operand(a, c, j0, width):
-            codes = tab_codes[c][:, a, j0 : j0 + width].bitcast(U8).bitcast(FP4X4)
+            codes = tab_codes[c][:, CHUNK * a + j0 : CHUNK * a + j0 + width].bitcast(U8).bitcast(FP4X4)
             scale_rows = picked_scales[:] if a == 0 else second_scales[:].bitcast(U8)
             return codes, scale_rows[:, CHUNK * c + j0 : CHUNK * c + j0 + width]
 
@@ -215,7 +224,7 @@ def tile_list_kvt_act_kernel(
             load(late.tile([P, 4, M], F32, name="x_raw", tag="x%d" % a, align_bytes=64)[:], x, a, 0, M) for a in range(2)
         ]
         wq_second = [
-            load(late.tile([P, 4, PASS], F32, name="wq_second", tag="wq%d" % b, align_bytes=64)[:], wq, 1, PASS * b, PASS)
+            load(late.tile([P, 4, PASS], F32, name="wq_second", tag="wq%d" % b, align_bytes=256)[:], wq, 1, PASS * b, PASS)
             for b in range(2)
         ]
 
@@ -263,10 +272,10 @@ def tile_list_kvt_act_kernel(
             else:
                 rows = ring.tile([P, 4 * CHUNK], BF16, name="key_rows%d" % n, align_bytes=64)
             key_rows[divmod(n, 4)] = rows
-        ka_scale_rows = late.tile([P, 2 * J], U8, name="ka_scales", tag="wq0", align_bytes=64)
-        ka_s = [ka_scale_rows[:, J * b : J * (b + 1)] for b in range(2)]
+        ka_scale_rows = late.tile([P, 2 * J + 192], U8, name="ka_scales", tag="wq0", align_bytes=256)
+        ka_s = [ka_scale_rows[:, 192 + J * b : 192 + J * (b + 1)] for b in range(2)]
         score_rows = [late.tile([P, J], F32, name="score_rows", tag="wk%d" % mt, align_bytes=64) for mt in range(4)]
-        query_rows = late.tile([P, 2, 4 * M], BF16, name="query_rows", tag="wq1", align_bytes=64)
+        query_rows = late.tile([P, 2, 4 * M], BF16, name="query_rows", tag="wq1", align_bytes=256)
 
         for n in range(7):
             keys(*divmod(n, 4))

@@ -133,8 +133,8 @@ def tile_list_kvt_act_kernel(
             bank = new_bank(CHUNK)
             for t in range(4):
                 two_passes(bank[:, P * t : P * (t + 1)], w_c, w_s, PASS * b + P * t, rhs_of_pass)
-            view_out = rows.rearrange("p (j i t) -> p j t i", t=4, i=2)
-            view_in = bank[:].rearrange("p (t j i) -> p j t i", t=4, i=2)
+            view_out = rows.rearrange("p (j t) -> p j t", t=4)
+            view_in = bank[:].rearrange("p (t j) -> p j t", t=4)
             if engine == "scalar":
                 nc.scalar.activation(view_out, view_in, RELU)
             else:

@@ -129,10 +129,7 @@ def tile_list_kvt_act_kernel(
                     stop=(a == 1),
                 )
 
-        def features(w_c, w_s, b, rhs_of_pass, engine, rows):
-            bank = new_bank(CHUNK)
-            for t in range(4):
-                two_passes(bank[:, P * t : P * (t + 1)], w_c, w_s, PASS * b + P * t, rhs_of_pass)
+        def empty_features(bank, engine, rows):
             view_out = rows.rearrange("p (j t) -> p j t", t=4)
             view_in = bank[:].rearrange("p (t j) -> p j t", t=4)
             if engine == "scalar":
@@ -140,13 +137,37 @@ def tile_list_kvt_act_kernel(
             else:
                 nc.vector.tensor_scalar(view_out, view_in, 0.0, None, MAX)
 
+        def features(w_c, w_s, b, rhs_of_pass, engine, rows):
+            bank = new_bank(CHUNK)
+            for t in range(4):
+                two_passes(bank[:, P * t : P * (t + 1)], w_c, w_s, PASS * b + P * t, rhs_of_pass)
+            empty_features(bank, engine, rows)
+
+        def first_keys(count):
+            banks = [new_bank(CHUNK) for s in range(count)]
+            for a in range(2):
+                for s in range(count):
+                    codes, scales = tab_operand(a, 0, P * s, P)
+                    for t in range(4):
+                        nc.tensor.matmul_mx(
+                            out=banks[s][:, P * t : P * (t + 1)],
+                            lhsT=wk_c[a][:, P * t : P * (t + 1)].bitcast(FP8X4),
+                            lhsT_scale=wk_s[a][:, P * t : P * (t + 1)],
+                            rhs=codes,
+                            rhs_scale=scales,
+                            start=(a == 0 and t == 0),
+                            stop=(a == 1 and t == 3),
+                        )
+                    if a == 1:
+                        empty_features(banks[s], "scalar", key_rows[0, 0][:, 4 * P * s : 4 * P * (s + 1)])
+
         def values(nt, c):
             bank = new_bank(CHUNK)
             two_passes(bank[:], wv_c, wv_s, P * nt, lambda a: tab_operand(a, c, 0, CHUNK))
             nc.scalar.copy(value_rows[nt][:, CHUNK * c : CHUNK * (c + 1)], bank[:])
 
-        def keys(b, c):
-            for s in range(4):
+        def keys(b, c, first=0):
+            for s in range(first, 4):
                 rows = key_rows[b, c][:, 4 * P * s : 4 * P * (s + 1)]
                 features(wk_c, wk_s, b, lambda a: tab_operand(a, c, P * s, P), "scalar", rows)
 
@@ -277,7 +298,9 @@ def tile_list_kvt_act_kernel(
         score_rows = [late.tile([P, J], F32, name="score_rows", tag="wk%d" % mt, align_bytes=64) for mt in range(4)]
         query_rows = late.tile([P, 2, 4 * M], BF16, name="query_rows", tag="wq1", align_bytes=256)
 
-        for n in range(7):
+        first_keys(3)
+        keys(0, 0, 3)
+        for n in range(1, 7):
             keys(*divmod(n, 4))
         for mt in range(4):
             queries(0, mt, "vector")

@@ -62,7 +62,7 @@ def tile_list_kvt_act_kernel(
                 [operand("%s_scales%d" % (name, a), U8, width, 1, scale_start) for a in range(2)],
             )
 
-        wv_c, wv_s = codes_pair("wv", N, 0, 64)
+        wv_ops = {}
         wk_c, wk_s = codes_pair("wk", R, 0, 64)
         wq_c, wq_s = codes_pair("wq", R, 0, 64)
         x_c, x_s = codes_pair("x", M, 128, 192)
@@ -116,8 +116,8 @@ def tile_list_kvt_act_kernel(
             scale_rows = picked_scales[:] if a == 0 else second_scales[:].bitcast(U8)
             return codes, scale_rows[:, CHUNK * c + j0 : CHUNK * c + j0 + width]
 
-        def two_passes(out, lhs_c, lhs_s, m0, rhs_of_pass):
-            for a in range(2):
+        def two_passes(out, lhs_c, lhs_s, m0, rhs_of_pass, order=(0, 1)):
+            for a in order:
                 codes, scales = rhs_of_pass(a)
                 nc.tensor.matmul_mx(
                     out=out,
@@ -125,8 +125,8 @@ def tile_list_kvt_act_kernel(
                     lhsT_scale=lhs_s[a][:, m0 : m0 + P],
                     rhs=codes,
                     rhs_scale=scales,
-                    start=(a == 0),
-                    stop=(a == 1),
+                    start=(a == order[0]),
+                    stop=(a == order[1]),
                 )
 
         def empty_features(bank, engine, rows):
@@ -147,7 +147,7 @@ def tile_list_kvt_act_kernel(
             banks = [new_bank(CHUNK) for s in range(count)]
             for a in range(2):
                 for s in range(count):
-                    codes, scales = tab_operand(a, 0, P * s, P)
+                    codes, scales = tab_operand(a, s // 4, P * (s % 4), P)
                     for t in range(4):
                         nc.tensor.matmul_mx(
                             out=banks[s][:, P * t : P * (t + 1)],
@@ -159,11 +159,14 @@ def tile_list_kvt_act_kernel(
                             stop=(a == 1 and t == 3),
                         )
                     if a == 1:
-                        empty_features(banks[s], "scalar", key_rows[0, 0][:, 4 * P * s : 4 * P * (s + 1)])
+                        empty_features(banks[s], "scalar", key_rows[0, s // 4][:, 4 * P * (s % 4) : 4 * P * (s % 4 + 1)])
 
         def values(nt, c):
             bank = new_bank(CHUNK)
-            two_passes(bank[:], wv_c, wv_s, P * nt, lambda a: tab_operand(a, c, 0, CHUNK))
+            lhs_c = [wv_ops[a, nt][0] for a in range(2)]
+            lhs_s = [wv_ops[a, nt][1] for a in range(2)]
+            order = (0, 1) if c == 0 and nt < 2 else (1, 0)
+            two_passes(bank[:], lhs_c, lhs_s, 0, lambda a: tab_operand(a, c, 0, CHUNK), order)
             nc.scalar.copy(value_rows[nt][:, CHUNK * c : CHUNK * (c + 1)], bank[:])
 
         def keys(b, c, first=0):
@@ -200,9 +203,19 @@ def tile_list_kvt_act_kernel(
             scores(mt, j0 + CHUNK, CHUNK, second)
             store_scores(mt, j0, 2 * CHUNK)
 
-        def wv_piece(a, c0, width):
+        def round_wv(a, c0, width):
             raw = wv_raw[a, c0 // HALF][:, :, c0 % HALF : c0 % HALF + width]
-            quantize(wv_c[a], wv_s[a], c0, width, round_plain("scalar", raw, width, "wv%d_%d" % (a, c0))[:])
+            return round_plain("scalar", raw, width, "wv%d_%d" % (a, c0))
+
+        def quantize_wv(a, c0, width, grouped):
+            codes = operand("wv_codes%d_%d" % (a, c0), U32, width, 4, 0)
+            scales = operand("wv_scales%d_%d" % (a, c0), U8, width, 1, 64)
+            quantize(codes, scales, 0, width, grouped[:])
+            for n in range(width // P):
+                wv_ops[a, c0 // P + n] = (codes[:, P * n : P * (n + 1)], scales[:, P * n : P * (n + 1)])
+
+        def wv_piece(a, c0, width):
+            quantize_wv(a, c0, width, round_wv(a, c0, width))
 
         def feature_weights(codes, scales, raw, a, b, tags=("cast", "cast")):
             halves = [round_permuted(raw, h, tags[h]) for h in range(2)]
@@ -227,7 +240,7 @@ def tile_list_kvt_act_kernel(
             for a in range(2):
                 low = arena.tile([P, 4, HALF], F32, name="wv_low%d" % a, offset=4 * T + 16 * HALF * a, align_bytes=64)
                 wv_raw[a, 0] = load(low[:], wv, a, 0, HALF)
-            wv_raw[0, 1] = load(ring.tile([P, 4, HALF], F32, name="wv_high0", align_bytes=64)[:], wv, 0, HALF, HALF)
+            wv_raw[0, 1] = load(ring.tile([P, 4, HALF], F32, name="wv_high0", tag="high0", align_bytes=256)[:], wv, 0, HALF, HALF)
             nc.vector.tensor_copy(picked_scales[:], table_scales[:].bitcast(U8).indirect(offsets[:]))
             picked_rows = picked_scales[:].bitcast(I32)
             for q in range(4):
@@ -254,13 +267,13 @@ def tile_list_kvt_act_kernel(
         wv_piece(1, 0, P)
         picked = gather_words(1, staging(U32, CHUNK, "wv1_0"))
         wv_piece(1, P, P)
+        upper = round_wv(0, HALF, HALF)
         part_words(1, picked, "wv1_128")
-        wv_piece(0, HALF, HALF)
-        picked = gather_words(2, staging(U32, CHUNK, "wv0_256"))
+        quantize_wv(0, HALF, HALF, upper)
         wv_piece(1, HALF, P)
         wv_piece(1, HALF + P, P)
-        part_words(2, picked, "wv1_256")
-        part_words(3, gather_words(3, staging(U32, CHUNK, "wv1_384")), "tab3")
+        for c in (2, 3):
+            part_words(c, gather_words(c, staging(U32, CHUNK, "wv1_384")), "tab%d" % c)
 
         first_rows = late.tile([P, 2, J], F32, name="first_rows", tag="high", align_bytes=64)
         value_rows = [first_rows[:, nt] for nt in range(2)]
@@ -298,9 +311,9 @@ def tile_list_kvt_act_kernel(
         score_rows = [late.tile([P, J], F32, name="score_rows", tag="wk%d" % mt, align_bytes=64) for mt in range(4)]
         query_rows = late.tile([P, 2, 4 * M], BF16, name="query_rows", tag="wq1", align_bytes=256)
 
-        first_keys(3)
-        keys(0, 0, 3)
-        for n in range(1, 7):
+        first_keys(5)
+        keys(0, 1, 1)
+        for n in range(2, 7):
             keys(*divmod(n, 4))
         for mt in range(4):
             queries(0, mt, "vector")

@@ -264,16 +264,17 @@ def tile_list_kvt_act_kernel(
 
         part_words(0, gather_words(0, staging(U32, CHUNK, "cast")), "tab0")
         wv_piece(0, 0, HALF)
+        picked = gather_words(1, staging(U32, CHUNK, "wv0_0"))
         wv_piece(1, 0, P)
-        picked = gather_words(1, staging(U32, CHUNK, "wv1_0"))
         wv_piece(1, P, P)
         upper = round_wv(0, HALF, HALF)
         part_words(1, picked, "wv1_128")
         quantize_wv(0, HALF, HALF, upper)
+        picked = gather_words(2, staging(U32, CHUNK, "wv0_256"))
         wv_piece(1, HALF, P)
         wv_piece(1, HALF + P, P)
-        for c in (2, 3):
-            part_words(c, gather_words(c, staging(U32, CHUNK, "wv1_384")), "tab%d" % c)
+        part_words(2, picked, "wv1_256")
+        part_words(3, gather_words(3, staging(U32, CHUNK, "wv1_384")), "tab3")
 
         first_rows = late.tile([P, 2, J], F32, name="first_rows", tag="high", align_bytes=64)
         value_rows = [first_rows[:, nt] for nt in range(2)]
@@ -311,8 +312,9 @@ def tile_list_kvt_act_kernel(
         score_rows = [late.tile([P, J], F32, name="score_rows", tag="wk%d" % mt, align_bytes=64) for mt in range(4)]
         query_rows = late.tile([P, 2, 4 * M], BF16, name="query_rows", tag="wq1", align_bytes=256)
 
-        first_keys(5)
-        keys(0, 1, 1)
+        first_keys(3)
+        keys(0, 0, 3)
+        keys(0, 1)
         for n in range(2, 7):
             keys(*divmod(n, 4))
         for mt in range(4):

@@ -175,7 +175,7 @@ def tile_list_kvt_act_kernel(
                 features(wk_c, wk_s, b, lambda a: tab_operand(a, c, P * s, P), "scalar", rows)
 
         def quantize_keys(b, c):
-            quantize(ka_c[b], ka_s[b], CHUNK * c, CHUNK, key_rows[b, c][:])
+            quantize(ka_c[b][:, CHUNK * c : CHUNK * (c + 1)], ka_s[b, c], 0, CHUNK, key_rows[b, c][:])
 
         def queries(b, mt, engine):
             cols = slice(P * mt, P * (mt + 1))
@@ -188,7 +188,10 @@ def tile_list_kvt_act_kernel(
         def scores(mt, j0, width, engine):
             cols = slice(j0, j0 + width)
             bank = new_bank(width)
-            two_passes(bank[:], qa_c, qa_s, P * mt, lambda b: (ka_c[b][:, cols].bitcast(FP8X4), ka_s[b][:, cols]))
+            c, first = divmod(j0, CHUNK)
+            two_passes(
+                bank[:], qa_c, qa_s, P * mt, lambda b: (ka_c[b][:, cols].bitcast(FP8X4), ka_s[b, c][:, first : first + width])
+            )
             if engine == "scalar":
                 nc.scalar.activation(score_rows[mt][:, cols], bank[:], COPY, scale=SCORE_SCALE)
             else:
@@ -253,10 +256,10 @@ def tile_list_kvt_act_kernel(
             for a in range(2):
                 raw = late.tile([P, 4, PASS], F32, name="wk_raw", tag="wk%d" % (2 * b + a), align_bytes=64)
                 wk_raw[a, b] = load(raw[:], wk, a, PASS * b, PASS)
-        wq_first = load(late.tile([P, 4, R], F32, name="wq_first")[:], wq, 0, 0, R)
         x_raw = [
-            load(late.tile([P, 4, M], F32, name="x_raw", tag="x%d" % a, align_bytes=64)[:], x, a, 0, M) for a in range(2)
+            load(late.tile([P, 4, M], F32, name="x_raw", tag="x%d" % a, align_bytes=256)[:], x, a, 0, M) for a in range(2)
         ]
+        wq_first = load(late.tile([P, 4, R], F32, name="wq_first")[:], wq, 0, 0, R)
         wq_second = [
             load(late.tile([P, 4, PASS], F32, name="wq_second", tag="wq%d" % b, align_bytes=256)[:], wq, 1, PASS * b, PASS)
             for b in range(2)
@@ -289,12 +292,12 @@ def tile_list_kvt_act_kernel(
         feature_weights(wk_c, wk_s, wk_raw[1, 0], 1, 0)
         for a in range(2):
             feature_weights(wk_c, wk_s, wk_raw[a, 1], a, 1)
-        for b in range(2):
-            feature_weights(wq_c, wq_s, wq_first[:, :, PASS * b : PASS * (b + 1)], 0, b)
         for a in range(2):
             halves = [round_plain("vector", x_raw[a][:, :, HALF * h : HALF * (h + 1)], HALF, "cast") for h in range(2)]
             for h in range(2):
                 quantize(x_c[a], x_s[a], HALF * h, HALF, halves[h][:])
+        for b in range(2):
+            feature_weights(wq_c, wq_s, wq_first[:, :, PASS * b : PASS * (b + 1)], 0, b)
         for b in range(2):
             feature_weights(wq_c, wq_s, wq_second[b], 1, b)
         for nt in range(4):
@@ -308,7 +311,12 @@ def tile_list_kvt_act_kernel(
                 rows = ring.tile([P, 4 * CHUNK], BF16, name="key_rows%d" % n, align_bytes=64)
             key_rows[divmod(n, 4)] = rows
         ka_scale_rows = late.tile([P, 2 * J + 192], U8, name="ka_scales", tag="wq0", align_bytes=256)
-        ka_s = [ka_scale_rows[:, 192 + J * b : 192 + J * (b + 1)] for b in range(2)]
+        ka_s = {}
+        for n in range(8):
+            ka_s[divmod(n, 4)] = ka_scale_rows[:, 192 + CHUNK * n : 192 + CHUNK * (n + 1)]
+        early_scale_rows = late.tile([P, 2 * CHUNK + 192], U8, name="ka_early_scales", tag="x1", align_bytes=256)
+        for c in range(2):
+            ka_s[0, c] = early_scale_rows[:, 192 + CHUNK * c : 192 + CHUNK * (c + 1)]
         score_rows = [late.tile([P, J], F32, name="score_rows", tag="wk%d" % mt, align_bytes=64) for mt in range(4)]
         query_rows = late.tile([P, 2, 4 * M], BF16, name="query_rows", tag="wq1", align_bytes=256)
 
@@ -317,29 +325,34 @@ def tile_list_kvt_act_kernel(
         keys(0, 1)
         for n in range(2, 7):
             keys(*divmod(n, 4))
-        for mt in range(4):
-            queries(0, mt, "vector")
-        keys(1, 3)
         for c in range(2):
             for b in range(2):
                 quantize_keys(b, c)
+        for mt in range(4):
+            queries(0, mt, ("vector", "scalar")[mt // 2])
         quantize_queries(0, 0, 4)
-        for mt in range(3):
-            queries(1, mt, ("vector", "scalar")[mt % 2])
+        for mt in range(4):
+            queries(1, mt, ("scalar", "vector")[mt % 2])
             quantize_queries(1, mt, 1)
-        score_pair(0, 0, "scalar")
-        queries(1, 3, "vector")
-        quantize_queries(1, 3, 1)
-        for c in (2, 3):
-            for b in range(2):
-                quantize_keys(b, c)
+        score_pair(0, 0, "vector")
         score_pair(1, 0, "scalar")
+        for b, c in ((0, 2), (1, 2), (0, 3)):
+            quantize_keys(b, c)
         score_pair(2, 0, "vector")
         score_pair(3, 0, "vector")
-        for mt in range(3):
-            score_pair(mt, 1, "vector")
-        scores(3, 2 * CHUNK, CHUNK, "scalar")
-        store_scores(3, 2 * CHUNK, CHUNK)
-        for h, engine in enumerate(("vector", "scalar")):
-            scores(3, 3 * CHUNK + HALF * h, HALF, engine)
-            store_scores(3, 3 * CHUNK + HALF * h, HALF)
+        scores(0, 2 * CHUNK, CHUNK, "scalar")
+        store_scores(0, 2 * CHUNK, CHUNK)
+        for s in range(4):
+            rows = key_rows[1, 3][:, 4 * P * s : 4 * P * (s + 1)]
+            features(wk_c, wk_s, 1, lambda a: tab_operand(a, 3, P * s, P), ("scalar", "vector")[s % 2], rows)
+            if s % 2 == 1:
+                first = HALF * (s // 2)
+                quantize(ka_c[1][:, 3 * CHUNK :], ka_s[1, 3], first, HALF, key_rows[1, 3][:, 4 * first : 4 * (first + HALF)])
+        last_tiles = [(mt, 2) for mt in range(1, 4)] + [(mt, 3) for mt in range(4)]
+        for n, (mt, c) in enumerate(last_tiles):
+            for h in range(2):
+                scores(mt, CHUNK * c + HALF * h, HALF, "vector" if h == 1 and n > 0 else "scalar")
+                if n == len(last_tiles) - 1:
+                    store_scores(mt, CHUNK * c + HALF * h, HALF)
+            if n < len(last_tiles) - 1:
+                store_scores(mt, CHUNK * c, CHUNK)

@@ -89,12 +89,14 @@ def tile_list_kvt_act_kernel(
                 nc.vector.tensor_copy(out, in_)
             return grouped
 
-        def round_permuted(raw, h, tag):
+        def round_permuted(engine, raw, h, tag):
             grouped = staging(BF16, 4 * HALF, tag)
-            nc.vector.tensor_copy(
-                grouped[:].rearrange("p (t c i j) -> p t c j i", t=2, i=4, j=4),
-                raw.rearrange("p j (c t i) -> p t c j i", t=4, i=4)[:, 2 * h : 2 * h + 2],
-            )
+            out = grouped[:].rearrange("p (t c i j) -> p t c j i", t=2, i=4, j=4)
+            in_ = raw.rearrange("p j (c t i) -> p t c j i", t=4, i=4)[:, 2 * h : 2 * h + 2]
+            if engine == "scalar":
+                nc.scalar.copy(out, in_)
+            else:
+                nc.vector.tensor_copy(out, in_)
             return grouped
 
         def quantize(codes, scales, c0, width, grouped):
@@ -106,13 +108,16 @@ def tile_list_kvt_act_kernel(
             nc.vector.tensor_copy(picked[:], table_words[:].bitcast(U32).indirect(offsets[:, 32 * c : 32 * (c + 1)]))
             return picked
 
-        def part_words(c, picked, tag):
-            padded = ring.tile([P, 2 * CHUNK + 64], U16, name="tab_codes", tag=tag, bufs=1, align_bytes=256)
-            tab_codes[c] = padded[:, 64:]
-            nc.vector.tensor_copy(tab_codes[c].rearrange("p (d j) -> p d j", d=2), picked[:].bitcast(U16).rearrange("p (j d) -> p d j", d=2))
+        def part_words(c, picked, tag, passes=(0, 1)):
+            count = len(passes)
+            padded = ring.tile([P, count * CHUNK + 64], U16, name="tab_codes", tag=tag, bufs=1, align_bytes=256)
+            words = picked[:].bitcast(U16).rearrange("p (j d) -> p d j", d=2)[:, passes[0] : passes[0] + count]
+            nc.vector.tensor_copy(padded[:, 64:].rearrange("p (d j) -> p d j", d=count), words)
+            for n, a in enumerate(passes):
+                tab_codes[a, c] = padded[:, 64 + CHUNK * n : 64 + CHUNK * (n + 1)]
 
         def tab_operand(a, c, j0, width):
-            codes = tab_codes[c][:, CHUNK * a + j0 : CHUNK * a + j0 + width].bitcast(U8).bitcast(FP4X4)
+            codes = tab_codes[a, c][:, j0 : j0 + width].bitcast(U8).bitcast(FP4X4)
             scale_rows = picked_scales[:] if a == 0 else second_scales[:].bitcast(U8)
             return codes, scale_rows[:, CHUNK * c + j0 : CHUNK * c + j0 + width]
 
@@ -161,13 +166,22 @@ def tile_list_kvt_act_kernel(
                     if a == 1:
                         empty_features(banks[s], "scalar", key_rows[0, s // 4][:, 4 * P * (s % 4) : 4 * P * (s % 4 + 1)])
 
-        def values(nt, c):
-            bank = new_bank(CHUNK)
-            lhs_c = [wv_ops[a, nt][0] for a in range(2)]
-            lhs_s = [wv_ops[a, nt][1] for a in range(2)]
-            order = (0, 1) if c == 0 and nt < 2 else (1, 0)
-            two_passes(bank[:], lhs_c, lhs_s, 0, lambda a: tab_operand(a, c, 0, CHUNK), order)
-            nc.scalar.copy(value_rows[nt][:, CHUNK * c : CHUNK * (c + 1)], bank[:])
+        def values(groups, order):
+            banks = [new_bank(CHUNK) for group in groups]
+            for a in order:
+                for bank, (nt, c) in zip(banks, groups):
+                    codes, scales = tab_operand(a, c, 0, CHUNK)
+                    nc.tensor.matmul_mx(
+                        out=bank[:],
+                        lhsT=wv_ops[a, nt][0].bitcast(FP8X4),
+                        lhsT_scale=wv_ops[a, nt][1],
+                        rhs=codes,
+                        rhs_scale=scales,
+                        start=(a == order[0]),
+                        stop=(a == order[1]),
+                    )
+                    if a == order[1]:
+                        nc.scalar.copy(value_rows[nt][:, CHUNK * c : CHUNK * (c + 1)], bank[:])
 
         def keys(b, c, first=0):
             for s in range(first, 4):
@@ -221,7 +235,7 @@ def tile_list_kvt_act_kernel(
             quantize_wv(a, c0, width, round_wv(a, c0, width))
 
         def feature_weights(codes, scales, raw, a, b, tags=("cast", "cast")):
-            halves = [round_permuted(raw, h, tags[h]) for h in range(2)]
+            halves = [round_permuted("vector", raw, h, tags[h]) for h in range(2)]
             for h in range(2):
                 quantize(codes[a], scales[a], PASS * b + HALF * h, HALF, halves[h][:])
 
@@ -243,13 +257,13 @@ def tile_list_kvt_act_kernel(
             for a in range(2):
                 low = arena.tile([P, 4, HALF], F32, name="wv_low%d" % a, offset=4 * T + 16 * HALF * a, align_bytes=64)
                 wv_raw[a, 0] = load(low[:], wv, a, 0, HALF)
-            wv_raw[0, 1] = load(ring.tile([P, 4, HALF], F32, name="wv_high0", tag="high0", align_bytes=256)[:], wv, 0, HALF, HALF)
             nc.vector.tensor_copy(picked_scales[:], table_scales[:].bitcast(U8).indirect(offsets[:]))
             picked_rows = picked_scales[:].bitcast(I32)
             for q in range(4):
                 nc.sync.dma_start(second_scales[32 * q : 32 * q + 4, :], picked_rows[32 * q + 4 : 32 * q + 32 : 8, :])
 
         late = ctx.enter_context(tc.tile_pool(name="late", bufs=1))
+        wv_raw[0, 1] = load(late.tile([P, 4, HALF], F32, name="wv_high0", align_bytes=64)[:], wv, 0, HALF, HALF)
         wv_raw[1, 1] = load(late.tile([P, 4, HALF], F32, name="wv_high1", tag="high", align_bytes=64)[:], wv, 1, HALF, HALF)
         wk_raw = {}
         for b in range(2):
@@ -265,30 +279,37 @@ def tile_list_kvt_act_kernel(
             for b in range(2)
         ]
 
-        part_words(0, gather_words(0, staging(U32, CHUNK, "cast")), "tab0")
-        wv_piece(0, 0, HALF)
-        picked = gather_words(1, staging(U32, CHUNK, "wv0_0"))
+        picked = gather_words(0, staging(U32, CHUNK, "cast"))
+        part_words(0, picked, "tab0", (0,))
+        wv_piece(0, 0, P)
+        wv_piece(0, P, P)
+        part_words(0, picked, "wv0_0", (1,))
         wv_piece(1, 0, P)
+        picked = gather_words(1, staging(U32, CHUNK, "wv1_0"))
         wv_piece(1, P, P)
         upper = round_wv(0, HALF, HALF)
         part_words(1, picked, "wv1_128")
         quantize_wv(0, HALF, HALF, upper)
         picked = gather_words(2, staging(U32, CHUNK, "wv0_256"))
-        wv_piece(1, HALF, P)
-        wv_piece(1, HALF + P, P)
+        wv_piece(1, HALF, HALF)
         part_words(2, picked, "wv1_256")
-        part_words(3, gather_words(3, staging(U32, CHUNK, "wv1_384")), "tab3")
+        part_words(3, gather_words(3, staging(U32, CHUNK, "wv0_256")), "tab3")
+        scalar_half = round_permuted("scalar", wk_raw[0, 0], 1, "wv1_0")
 
         first_rows = late.tile([P, 2, J], F32, name="first_rows", tag="high", align_bytes=64)
         value_rows = [first_rows[:, nt] for nt in range(2)]
         value_rows.extend(ring.tile([P, J], F32, name="value_rows%d" % nt)[:] for nt in (2, 3))
-        for chunks in ((0, 1), (2,), (3,)):
-            for first_tile in (0, 2):
-                for c in chunks:
-                    values(first_tile, c)
-                    values(first_tile + 1, c)
+        values([(0, 0), (1, 0)], (0, 1))
+        for nt in range(2):
+            values([(nt, 1)], (1, 0))
+        values([(2, 0), (3, 0), (2, 1), (3, 1)], (0, 1))
+        for c in (2, 3):
+            for nt in range(4):
+                values([(nt, c)], (1, 0))
 
-        feature_weights(wk_c, wk_s, wk_raw[0, 0], 0, 0, ("wv1_384", "cast"))
+        vector_half = round_permuted("vector", wk_raw[0, 0], 0, "cast")
+        quantize(wk_c[0], wk_s[0], HALF, HALF, scalar_half[:])
+        quantize(wk_c[0], wk_s[0], 0, HALF, vector_half[:])
         feature_weights(wk_c, wk_s, wk_raw[1, 0], 1, 0)
         for a in range(2):
             feature_weights(wk_c, wk_s, wk_raw[a, 1], a, 1)

@@ -23,6 +23,7 @@ PASS = 512
 CHUNK = 512
 HALF = 256
 BANKS = 8
+BANK_BYTES = 2048
 CAST_BUFS = 4
 KEY_ROW_BYTES = 8 * CHUNK
 ARENA_KEY_ROWS = 6
@@ -41,7 +42,12 @@ def tile_list_kvt_act_kernel(
 
         def new_bank(width):
             banks_taken.append(len(banks_taken) % BANKS)
-            return psum.tile([P, width], F32, name="bank", tag="bank%d" % banks_taken[-1])
+            return psum.tile([P, width], F32, name="bank%d" % len(banks_taken), offset=BANK_BYTES * banks_taken[-1])
+
+        def new_bank_pair():
+            banks_taken.extend([len(banks_taken) % BANKS, len(banks_taken) % BANKS + 1])
+            pair = psum.tile([P, 2 * CHUNK], F32, name="pair%d" % len(banks_taken), offset=BANK_BYTES * banks_taken[-2])
+            return [pair[:, CHUNK * s : CHUNK * (s + 1)] for s in range(2)]
 
         offsets = keep.tile([P, J // 16], U16, name="offsets")
         arena = ctx.enter_context(tc.tile_pool(name="arena", bufs=1))
@@ -66,7 +72,8 @@ def tile_list_kvt_act_kernel(
         wk_c, wk_s = codes_pair("wk", R, 0, 64)
         wq_c, wq_s = codes_pair("wq", R, 0, 64)
         x_c, x_s = codes_pair("x", M, 128, 192)
-        qa_c, qa_s = codes_pair("qa", M, 0, 64)
+        qa_c = operand("qa_codes", U32, 2 * M, 4, 0)
+        qa_s = operand("qa_scales", U8, 2 * M, 1, 64)
         ka_c = [operand("ka_codes%d" % b, U32, J, 4, 128) for b in range(2)]
         picked_scales = operand("picked_scales", U8, J, 1, 192)
         second_scales = operand("second_scales", I32, J // 4, 4, 192)
@@ -136,35 +143,56 @@ def tile_list_kvt_act_kernel(
 
         def empty_features(bank, engine, rows):
             view_out = rows.rearrange("p (j t) -> p j t", t=4)
-            view_in = bank[:].rearrange("p (t j) -> p j t", t=4)
+            view_in = bank.rearrange("p (t j) -> p j t", t=4)
             if engine == "scalar":
                 nc.scalar.activation(view_out, view_in, RELU)
             else:
                 nc.vector.tensor_scalar(view_out, view_in, 0.0, None, MAX)
 
-        def features(w_c, w_s, b, rhs_of_pass, engine, rows):
+        def features(w_c, w_s, b, rhs_of_pass):
             bank = new_bank(CHUNK)
             for t in range(4):
                 two_passes(bank[:, P * t : P * (t + 1)], w_c, w_s, PASS * b + P * t, rhs_of_pass)
-            empty_features(bank, engine, rows)
+            return bank[:]
 
-        def first_keys(count):
-            banks = [new_bank(CHUNK) for s in range(count)]
-            for a in range(2):
-                for s in range(count):
-                    codes, scales = tab_operand(a, s // 4, P * (s % 4), P)
-                    for t in range(4):
+        def feature_pair(w_c, w_s, b, rhs_of_bank):
+            banks = new_bank_pair()
+            for t in range(4):
+                cols = slice(PASS * b + P * t, PASS * b + P * (t + 1))
+                for a in range(2):
+                    for s in range(2):
+                        codes, scales = rhs_of_bank(s, a)
                         nc.tensor.matmul_mx(
                             out=banks[s][:, P * t : P * (t + 1)],
-                            lhsT=wk_c[a][:, P * t : P * (t + 1)].bitcast(FP8X4),
-                            lhsT_scale=wk_s[a][:, P * t : P * (t + 1)],
+                            lhsT=w_c[a][:, cols].bitcast(FP8X4),
+                            lhsT_scale=w_s[a][:, cols],
                             rhs=codes,
                             rhs_scale=scales,
-                            start=(a == 0 and t == 0),
-                            stop=(a == 1 and t == 3),
+                            start=(a == 0),
+                            stop=(a == 1),
                         )
+            return banks
+
+        def first_keys(count):
+            pairs = [new_bank_pair() for u in range(count)]
+            for a in range(2):
+                for u in range(count):
+                    for t in range(4):
+                        for s in range(2):
+                            codes, scales = tab_operand(a, 0, P * (2 * u + s), P)
+                            nc.tensor.matmul_mx(
+                                out=pairs[u][s][:, P * t : P * (t + 1)],
+                                lhsT=wk_c[a][:, P * t : P * (t + 1)].bitcast(FP8X4),
+                                lhsT_scale=wk_s[a][:, P * t : P * (t + 1)],
+                                rhs=codes,
+                                rhs_scale=scales,
+                                start=(a == 0 and t == 0),
+                                stop=(a == 1 and t == 3),
+                            )
                     if a == 1:
-                        empty_features(banks[s], "scalar", key_rows[0, s // 4][:, 4 * P * (s % 4) : 4 * P * (s % 4 + 1)])
+                        for s in range(2):
+                            n = 2 * u + s
+                            empty_features(pairs[u][s], "scalar", key_rows[0, 0][:, 4 * P * n : 4 * P * (n + 1)])
 
         def values(groups, order):
             banks = [new_bank(CHUNK) for group in groups]
@@ -183,28 +211,33 @@ def tile_list_kvt_act_kernel(
                     if a == order[1]:
                         nc.scalar.copy(value_rows[nt][:, CHUNK * c : CHUNK * (c + 1)], bank[:])
 
-        def keys(b, c, first=0):
-            for s in range(first, 4):
-                rows = key_rows[b, c][:, 4 * P * s : 4 * P * (s + 1)]
-                features(wk_c, wk_s, b, lambda a: tab_operand(a, c, P * s, P), "scalar", rows)
+        def keys(b, c):
+            for u in range(2):
+                banks = feature_pair(wk_c, wk_s, b, lambda s, a: tab_operand(a, c, P * (2 * u + s), P))
+                for s in range(2):
+                    empty_features(banks[s], "scalar", key_rows[b, c][:, 4 * P * (2 * u + s) : 4 * P * (2 * u + s + 1)])
 
         def quantize_keys(b, c):
             quantize(ka_c[b][:, CHUNK * c : CHUNK * (c + 1)], ka_s[b, c], 0, CHUNK, key_rows[b, c][:])
 
-        def queries(b, mt, engine):
+        def queries(b, mt):
             cols = slice(P * mt, P * (mt + 1))
-            rows = query_rows[:, b, 4 * P * mt : 4 * P * (mt + 1)]
-            features(wq_c, wq_s, b, lambda a: (x_c[a][:, cols].bitcast(FP8X4), x_s[a][:, cols]), engine, rows)
+            return features(wq_c, wq_s, b, lambda a: (x_c[a][:, cols].bitcast(FP8X4), x_s[a][:, cols]))
 
-        def quantize_queries(b, mt, count):
-            quantize(qa_c[b], qa_s[b], P * mt, P * count, query_rows[:, b, 4 * P * mt : 4 * P * (mt + count)])
+        def empty_queries(b, mt, engine):
+            empty_features(query_banks[b, mt], engine, query_rows[:, mt, 4 * P * b : 4 * P * (b + 1)])
+
+        def quantize_queries(mt):
+            quantize(qa_c, qa_s, 2 * P * mt, 2 * P, query_rows[:, mt])
 
         def scores(mt, j0, width, engine):
             cols = slice(j0, j0 + width)
             bank = new_bank(width)
             c, first = divmod(j0, CHUNK)
+            lhs_c = [qa_c[:, P * b :] for b in range(2)]
+            lhs_s = [qa_s[:, P * b :] for b in range(2)]
             two_passes(
-                bank[:], qa_c, qa_s, P * mt, lambda b: (ka_c[b][:, cols].bitcast(FP8X4), ka_s[b, c][:, first : first + width])
+                bank[:], lhs_c, lhs_s, 2 * P * mt, lambda b: (ka_c[b][:, cols].bitcast(FP8X4), ka_s[b, c][:, first : first + width])
             )
             if engine == "scalar":
                 nc.scalar.activation(score_rows[mt][:, cols], bank[:], COPY, scale=SCORE_SCALE)
@@ -242,10 +275,6 @@ def tile_list_kvt_act_kernel(
         with tc.tile_pool(name="early", bufs=1) as early:
             table_scales = early.tile([P, T // 4], I32, name="table_scales")
             nc.vector.memset(second_scales[:], 0)
-            warm_in = keep.tile([P, 8], F32, name="warm_in")
-            warm_out = keep.tile([P, 8], F32, name="warm_out")
-            nc.vector.memset(warm_in[:], 0.0)
-            nc.scalar.activation(warm_out[:], warm_in[:], RELU)
             nc.sync.dma_start(offsets[:], offs)
             scale_rows_hbm = tab_scales.rearrange("a q t -> (a q) t").bitcast(I32)
             nc.sync.dma_start(table_scales[0:P:4, :], tab_scales.rearrange("a q t -> q a t").bitcast(I32))
@@ -257,14 +286,14 @@ def tile_list_kvt_act_kernel(
             for a in range(2):
                 low = arena.tile([P, 4, HALF], F32, name="wv_low%d" % a, offset=4 * T + 16 * HALF * a, align_bytes=64)
                 wv_raw[a, 0] = load(low[:], wv, a, 0, HALF)
+            wv_raw[1, 1] = load(ring.tile([P, 4, HALF], F32, name="wv_high1", align_bytes=256)[:], wv, 1, HALF, HALF)
             nc.vector.tensor_copy(picked_scales[:], table_scales[:].bitcast(U8).indirect(offsets[:]))
             picked_rows = picked_scales[:].bitcast(I32)
             for q in range(4):
                 nc.sync.dma_start(second_scales[32 * q : 32 * q + 4, :], picked_rows[32 * q + 4 : 32 * q + 32 : 8, :])
 
         late = ctx.enter_context(tc.tile_pool(name="late", bufs=1))
-        wv_raw[0, 1] = load(late.tile([P, 4, HALF], F32, name="wv_high0", align_bytes=64)[:], wv, 0, HALF, HALF)
-        wv_raw[1, 1] = load(late.tile([P, 4, HALF], F32, name="wv_high1", tag="high", align_bytes=64)[:], wv, 1, HALF, HALF)
+        wv_raw[0, 1] = load(late.tile([P, 4, HALF], F32, name="wv_high0", tag="high", align_bytes=64)[:], wv, 0, HALF, HALF)
         wk_raw = {}
         for b in range(2):
             for a in range(2):
@@ -282,19 +311,19 @@ def tile_list_kvt_act_kernel(
         picked = gather_words(0, staging(U32, CHUNK, "cast"))
         part_words(0, picked, "tab0", (0,))
         wv_piece(0, 0, P)
+        picked_next = gather_words(1, staging(U32, CHUNK, "wv0_0"))
         wv_piece(0, P, P)
-        part_words(0, picked, "wv0_0", (1,))
+        part_words(0, picked, "wv0_128", (1,))
+        picked = picked_next
         wv_piece(1, 0, P)
-        picked = gather_words(1, staging(U32, CHUNK, "wv1_0"))
         wv_piece(1, P, P)
-        upper = round_wv(0, HALF, HALF)
+        upper = round_wv(1, HALF, HALF)
         part_words(1, picked, "wv1_128")
-        quantize_wv(0, HALF, HALF, upper)
-        picked = gather_words(2, staging(U32, CHUNK, "wv0_256"))
-        wv_piece(1, HALF, HALF)
-        part_words(2, picked, "wv1_256")
-        part_words(3, gather_words(3, staging(U32, CHUNK, "wv0_256")), "tab3")
-        scalar_half = round_permuted("scalar", wk_raw[0, 0], 1, "wv1_0")
+        quantize_wv(1, HALF, HALF, upper)
+        picked = gather_words(2, staging(U32, CHUNK, "wv1_256"))
+        wv_piece(0, HALF, HALF)
+        part_words(2, picked, "wv0_256")
+        part_words(3, gather_words(3, staging(U32, CHUNK, "wv1_256")), "tab3")
 
         first_rows = late.tile([P, 2, J], F32, name="first_rows", tag="high", align_bytes=64)
         value_rows = [first_rows[:, nt] for nt in range(2)]
@@ -302,14 +331,12 @@ def tile_list_kvt_act_kernel(
         values([(0, 0), (1, 0)], (0, 1))
         for nt in range(2):
             values([(nt, 1)], (1, 0))
-        values([(2, 0), (3, 0), (2, 1), (3, 1)], (0, 1))
+        values([(2, 0), (3, 0), (2, 1), (3, 1)], (1, 0))
         for c in (2, 3):
             for nt in range(4):
                 values([(nt, c)], (1, 0))
 
-        vector_half = round_permuted("vector", wk_raw[0, 0], 0, "cast")
-        quantize(wk_c[0], wk_s[0], HALF, HALF, scalar_half[:])
-        quantize(wk_c[0], wk_s[0], 0, HALF, vector_half[:])
+        feature_weights(wk_c, wk_s, wk_raw[0, 0], 0, 0)
         feature_weights(wk_c, wk_s, wk_raw[1, 0], 1, 0)
         for a in range(2):
             feature_weights(wk_c, wk_s, wk_raw[a, 1], a, 1)
@@ -331,41 +358,53 @@ def tile_list_kvt_act_kernel(
             else:
                 rows = ring.tile([P, 4 * CHUNK], BF16, name="key_rows%d" % n, align_bytes=64)
             key_rows[divmod(n, 4)] = rows
-        ka_scale_rows = late.tile([P, 2 * J + 192], U8, name="ka_scales", tag="wq0", align_bytes=256)
         ka_s = {}
-        for n in range(8):
-            ka_s[divmod(n, 4)] = ka_scale_rows[:, 192 + CHUNK * n : 192 + CHUNK * (n + 1)]
-        early_scale_rows = late.tile([P, 2 * CHUNK + 192], U8, name="ka_early_scales", tag="x1", align_bytes=256)
-        for c in range(2):
-            ka_s[0, c] = early_scale_rows[:, 192 + CHUNK * c : 192 + CHUNK * (c + 1)]
-        score_rows = [late.tile([P, J], F32, name="score_rows", tag="wk%d" % mt, align_bytes=64) for mt in range(4)]
-        query_rows = late.tile([P, 2, 4 * M], BF16, name="query_rows", tag="wq1", align_bytes=256)
 
-        first_keys(3)
-        keys(0, 0, 3)
+        def key_scales(name, tag, chunks):
+            rows = late.tile([P, len(chunks) * CHUNK + 192], U8, name=name, tag=tag, align_bytes=256)
+            for n, chunk in enumerate(chunks):
+                ka_s[chunk] = rows[:, 192 + CHUNK * n : 192 + CHUNK * (n + 1)]
+
+        key_scales("ka_middle_scales", "wq0", [(1, 0), (1, 1)])
+        key_scales("ka_early_scales", "x1", [(0, 0), (0, 1)])
+        score_rows = [late.tile([P, J], F32, name="score_rows", tag="wk%d" % mt, align_bytes=64) for mt in range(4)]
+        query_rows = late.tile([P, 4, 8 * P], BF16, name="query_rows", tag="wq1", align_bytes=256)
+
+        first_keys(2)
         keys(0, 1)
         for n in range(2, 7):
             keys(*divmod(n, 4))
         for c in range(2):
-            for b in range(2):
-                quantize_keys(b, c)
-        for mt in range(4):
-            queries(0, mt, ("vector", "scalar")[mt // 2])
-        quantize_queries(0, 0, 4)
-        for mt in range(4):
-            queries(1, mt, ("scalar", "vector")[mt % 2])
-            quantize_queries(1, mt, 1)
-        score_pair(0, 0, "vector")
+            quantize_keys(0, c)
+        query_banks = {(b, mt): queries(b, mt) for b in range(2) for mt in range(4)}
+        quantize_keys(1, 0)
+        empty_queries(0, 0, "vector")
+        empty_queries(1, 0, "scalar")
+        quantize_keys(1, 1)
+        quantize_queries(0)
+        empty_queries(0, 1, "vector")
+        empty_queries(1, 1, "scalar")
+        for b in range(2):
+            empty_queries(b, 2, "scalar")
+        empty_queries(0, 3, "vector")
+        quantize_queries(1)
+        empty_queries(1, 3, "vector")
+        quantize_queries(2)
+        quantize_queries(3)
+        key_scales("ka_late_scales", "wq1", [(0, 2), (1, 2), (0, 3), (1, 3)])
+        score_pair(0, 0, "scalar")
+        quantize_keys(0, 2)
         score_pair(1, 0, "scalar")
-        for b, c in ((0, 2), (1, 2), (0, 3)):
-            quantize_keys(b, c)
-        score_pair(2, 0, "vector")
+        quantize_keys(1, 2)
+        quantize_keys(0, 3)
+        score_pair(2, 0, "scalar")
         score_pair(3, 0, "vector")
         scores(0, 2 * CHUNK, CHUNK, "scalar")
         store_scores(0, 2 * CHUNK, CHUNK)
         for s in range(4):
             rows = key_rows[1, 3][:, 4 * P * s : 4 * P * (s + 1)]
-            features(wk_c, wk_s, 1, lambda a: tab_operand(a, 3, P * s, P), ("scalar", "vector")[s % 2], rows)
+            bank = features(wk_c, wk_s, 1, lambda a: tab_operand(a, 3, P * s, P))
+            empty_features(bank, ("scalar", "vector")[s % 2], rows)
             if s % 2 == 1:
                 first = HALF * (s // 2)
                 quantize(ka_c[1][:, 3 * CHUNK :], ka_s[1, 3], first, HALF, key_rows[1, 3][:, 4 * first : 4 * (first + HALF)])

@@ -217,6 +217,28 @@ def tile_list_kvt_act_kernel(
                 for s in range(2):
                     empty_features(banks[s], "scalar", key_rows[b, c][:, 4 * P * (2 * u + s) : 4 * P * (2 * u + s + 1)])
 
+        def wide_keys(b, c):
+            for u in range(2):
+                for h in range(2):
+                    bank = new_bank(CHUNK)
+                    for t in range(2):
+                        out = bank[:, HALF * t : HALF * (t + 1)]
+                        two_passes(out, wk_c, wk_s, PASS * b + P * (2 * h + t), lambda a: tab_operand(a, c, HALF * u, HALF))
+                    first = 2 * (CHUNK * h + HALF * u)
+                    pairs = key_rows[b, c][:, first : first + 2 * HALF].rearrange("p (j t) -> p j t", t=2)
+                    nc.scalar.activation(pairs, bank[:].rearrange("p (t j) -> p j t", t=2), RELU)
+
+        def weave_keys(b, c, woven):
+            words = key_rows[b, c][:].bitcast(I32).rearrange("p (h j) -> p j h", h=2)
+            nc.vector.tensor_copy(woven.rearrange("p (j h) -> p j h", h=2), words)
+            return woven.bitcast(BF16)
+
+        def woven_rows():
+            return late.tile([P, 2 * CHUNK], I32, name="woven", tag="x0", align_bytes=256)[:]
+
+        def quantize_woven(b, c, woven):
+            quantize(ka_c[b][:, CHUNK * c : CHUNK * (c + 1)], ka_s[b, c], 0, CHUNK, woven)
+
         def quantize_keys(b, c):
             quantize(ka_c[b][:, CHUNK * c : CHUNK * (c + 1)], ka_s[b, c], 0, CHUNK, key_rows[b, c][:])
 
@@ -356,7 +378,7 @@ def tile_list_kvt_act_kernel(
             if n < ARENA_KEY_ROWS:
                 rows = arena.tile([P, 4 * CHUNK], BF16, name="key_rows%d" % n, offset=KEY_ROW_BYTES * n, align_bytes=64)
             else:
-                rows = ring.tile([P, 4 * CHUNK], BF16, name="key_rows%d" % n, align_bytes=64)
+                rows = ring.tile([P, 4 * CHUNK], BF16, name="key_rows", tag="key_rows%d" % n, align_bytes=64)
             key_rows[divmod(n, 4)] = rows
         ka_s = {}
 
@@ -373,9 +395,13 @@ def tile_list_kvt_act_kernel(
         first_keys(2)
         keys(0, 1)
         for n in range(2, 7):
-            keys(*divmod(n, 4))
+            if n % 4 < 2:
+                keys(*divmod(n, 4))
+            else:
+                wide_keys(*divmod(n, 4))
         for c in range(2):
             quantize_keys(0, c)
+        woven = weave_keys(0, 2, woven_rows())
         query_banks = {(b, mt): queries(b, mt) for b in range(2) for mt in range(4)}
         quantize_keys(1, 0)
         empty_queries(0, 0, "vector")
@@ -393,10 +419,12 @@ def tile_list_kvt_act_kernel(
         quantize_queries(3)
         key_scales("ka_late_scales", "wq1", [(0, 2), (1, 2), (0, 3), (1, 3)])
         score_pair(0, 0, "scalar")
-        quantize_keys(0, 2)
+        quantize_woven(0, 2, woven)
         score_pair(1, 0, "scalar")
-        quantize_keys(1, 2)
-        quantize_keys(0, 3)
+        upper_woven = weave_keys(1, 2, woven_rows())
+        woven = weave_keys(0, 3, ring.tile([P, 2 * CHUNK], I32, name="woven", tag="key_rows6", align_bytes=64)[:])
+        quantize_woven(1, 2, upper_woven)
+        quantize_woven(0, 3, woven)
         score_pair(2, 0, "scalar")
         score_pair(3, 0, "vector")
         scores(0, 2 * CHUNK, CHUNK, "scalar")

@@ -217,24 +217,32 @@ def tile_list_kvt_act_kernel(
                 for s in range(2):
                     empty_features(banks[s], "scalar", key_rows[b, c][:, 4 * P * (2 * u + s) : 4 * P * (2 * u + s + 1)])
 
-        def wide_keys(b, c):
+        def wide_keys(b, c, upper_engine):
             for u in range(2):
                 for h in range(2):
                     bank = new_bank(CHUNK)
                     for t in range(2):
                         out = bank[:, HALF * t : HALF * (t + 1)]
                         two_passes(out, wk_c, wk_s, PASS * b + P * (2 * h + t), lambda a: tab_operand(a, c, HALF * u, HALF))
-                    first = 2 * (CHUNK * h + HALF * u)
-                    pairs = key_rows[b, c][:, first : first + 2 * HALF].rearrange("p (j t) -> p j t", t=2)
-                    nc.scalar.activation(pairs, bank[:].rearrange("p (t j) -> p j t", t=2), RELU)
+                    pairs = pair_rows[b, c, u][:, 2 * HALF * h : 2 * HALF * (h + 1)].rearrange("p (j t) -> p j t", t=2)
+                    sums = bank[:].rearrange("p (t j) -> p j t", t=2)
+                    if u == 0 or upper_engine == "scalar":
+                        nc.scalar.activation(pairs, sums, RELU)
+                    else:
+                        nc.vector.tensor_scalar(pairs, sums, 0.0, None, MAX)
 
         def weave_keys(b, c, woven):
-            words = key_rows[b, c][:].bitcast(I32).rearrange("p (h j) -> p j h", h=2)
-            nc.vector.tensor_copy(woven.rearrange("p (j h) -> p j h", h=2), words)
+            if (b, c) == (0, 2):
+                for u in range(2):
+                    words = pair_rows[b, c, u].bitcast(I32).rearrange("p (h j) -> p j h", h=2)
+                    nc.vector.tensor_copy(woven[:, CHUNK * u : CHUNK * (u + 1)].rearrange("p (j h) -> p j h", h=2), words)
+            else:
+                words = key_rows[b, c][:].bitcast(I32).rearrange("p (u h j) -> p u j h", u=2, h=2)
+                nc.vector.tensor_copy(woven.rearrange("p (u j h) -> p u j h", u=2, h=2), words)
             return woven.bitcast(BF16)
 
-        def woven_rows():
-            return late.tile([P, 2 * CHUNK], I32, name="woven", tag="x0", align_bytes=256)[:]
+        def woven_rows(tag):
+            return late.tile([P, 2 * CHUNK], I32, name="woven", tag=tag, align_bytes=256)[:]
 
         def quantize_woven(b, c, woven):
             quantize(ka_c[b][:, CHUNK * c : CHUNK * (c + 1)], ka_s[b, c], 0, CHUNK, woven)
@@ -247,10 +255,10 @@ def tile_list_kvt_act_kernel(
             return features(wq_c, wq_s, b, lambda a: (x_c[a][:, cols].bitcast(FP8X4), x_s[a][:, cols]))
 
         def empty_queries(b, mt, engine):
-            empty_features(query_banks[b, mt], engine, query_rows[:, mt, 4 * P * b : 4 * P * (b + 1)])
+            empty_features(query_banks[b, mt], engine, query_rows[mt][:, 4 * P * b : 4 * P * (b + 1)])
 
         def quantize_queries(mt):
-            quantize(qa_c, qa_s, 2 * P * mt, 2 * P, query_rows[:, mt])
+            quantize(qa_c, qa_s, 2 * P * mt, 2 * P, query_rows[mt][:])
 
         def scores(mt, j0, width, engine):
             cols = slice(j0, j0 + width)
@@ -324,7 +332,7 @@ def tile_list_kvt_act_kernel(
         x_raw = [
             load(late.tile([P, 4, M], F32, name="x_raw", tag="x%d" % a, align_bytes=256)[:], x, a, 0, M) for a in range(2)
         ]
-        wq_first = load(late.tile([P, 4, R], F32, name="wq_first")[:], wq, 0, 0, R)
+        wq_first = load(late.tile([P, 4, R], F32, name="wq_first", tag="wq_first", align_bytes=256)[:], wq, 0, 0, R)
         wq_second = [
             load(late.tile([P, 4, PASS], F32, name="wq_second", tag="wq%d" % b, align_bytes=256)[:], wq, 1, PASS * b, PASS)
             for b in range(2)
@@ -363,16 +371,10 @@ def tile_list_kvt_act_kernel(
         for a in range(2):
             feature_weights(wk_c, wk_s, wk_raw[a, 1], a, 1)
         for a in range(2):
-            halves = [round_plain("vector", x_raw[a][:, :, HALF * h : HALF * (h + 1)], HALF, "cast") for h in range(2)]
+            tags = ("cast", ("cast", "wv1_256")[a])
+            halves = [round_plain("vector", x_raw[a][:, :, HALF * h : HALF * (h + 1)], HALF, tags[h]) for h in range(2)]
             for h in range(2):
                 quantize(x_c[a], x_s[a], HALF * h, HALF, halves[h][:])
-        for b in range(2):
-            feature_weights(wq_c, wq_s, wq_first[:, :, PASS * b : PASS * (b + 1)], 0, b)
-        for b in range(2):
-            feature_weights(wq_c, wq_s, wq_second[b], 1, b)
-        for nt in range(4):
-            nc.sync.dma_start(out_1[P * nt : P * (nt + 1), :], value_rows[nt])
-
         key_rows = {}
         for n in range(8):
             if n < ARENA_KEY_ROWS:
@@ -380,6 +382,12 @@ def tile_list_kvt_act_kernel(
             else:
                 rows = ring.tile([P, 4 * CHUNK], BF16, name="key_rows", tag="key_rows%d" % n, align_bytes=64)
             key_rows[divmod(n, 4)] = rows
+        pair_rows = {
+            (b, c, u): key_rows[b, c][:, 2 * CHUNK * u : 2 * CHUNK * (u + 1)]
+            for b, c in [(0, 2), (0, 3), (1, 2)]
+            for u in range(2)
+        }
+        pair_rows[0, 2, 1] = late.tile([P, 2 * CHUNK], BF16, name="pair_rows", tag="x1", align_bytes=256)[:]
         ka_s = {}
 
         def key_scales(name, tag, chunks):
@@ -387,27 +395,40 @@ def tile_list_kvt_act_kernel(
             for n, chunk in enumerate(chunks):
                 ka_s[chunk] = rows[:, 192 + CHUNK * n : 192 + CHUNK * (n + 1)]
 
-        key_scales("ka_middle_scales", "wq0", [(1, 0), (1, 1)])
-        key_scales("ka_early_scales", "x1", [(0, 0), (0, 1)])
-        score_rows = [late.tile([P, J], F32, name="score_rows", tag="wk%d" % mt, align_bytes=64) for mt in range(4)]
-        query_rows = late.tile([P, 4, 8 * P], BF16, name="query_rows", tag="wq1", align_bytes=256)
-
+        early_scales = staging(U8, 2 * CHUNK + 192, "wv1_256")
+        for c in range(2):
+            ka_s[0, c] = early_scales[:, 192 + CHUNK * c : 192 + CHUNK * (c + 1)]
         first_keys(2)
         keys(0, 1)
-        for n in range(2, 7):
-            if n % 4 < 2:
-                keys(*divmod(n, 4))
-            else:
-                wide_keys(*divmod(n, 4))
+        wide_keys(0, 2, "vector")
         for c in range(2):
             quantize_keys(0, c)
-        woven = weave_keys(0, 2, woven_rows())
+        for b in range(2):
+            feature_weights(wq_c, wq_s, wq_first[:, :, PASS * b : PASS * (b + 1)], 0, b)
+        for b in range(2):
+            feature_weights(wq_c, wq_s, wq_second[b], 1, b, (("cast", "wv0_0")[b], "cast"))
+        for nt in range(4):
+            nc.sync.dma_start(out_1[P * nt : P * (nt + 1), :], value_rows[nt])
+
+        key_scales("ka_middle_scales", "wq0", [(1, 0), (1, 1)])
+        score_rows = [late.tile([P, J], F32, name="score_rows", tag="wk%d" % mt, align_bytes=64) for mt in range(4)]
+        query_rows = {
+            0: late.tile([P, 8 * P], BF16, name="query_rows0", tag="wq1", align_bytes=256),
+            1: staging(BF16, 8 * P, "wv0_0"),
+            2: late.tile([P, 8 * P], BF16, name="query_rows2", tag="wq_first", align_bytes=256),
+        }
+
+        wide_keys(0, 3, "scalar")
+        keys(1, 0)
+        keys(1, 1)
+        wide_keys(1, 2, "scalar")
         query_banks = {(b, mt): queries(b, mt) for b in range(2) for mt in range(4)}
         quantize_keys(1, 0)
         empty_queries(0, 0, "vector")
         empty_queries(1, 0, "scalar")
         quantize_keys(1, 1)
         quantize_queries(0)
+        query_rows[3] = late.tile([P, 8 * P], BF16, name="query_rows3", tag="wq1", align_bytes=256)
         empty_queries(0, 1, "vector")
         empty_queries(1, 1, "scalar")
         for b in range(2):
@@ -418,12 +439,14 @@ def tile_list_kvt_act_kernel(
         quantize_queries(2)
         quantize_queries(3)
         key_scales("ka_late_scales", "wq1", [(0, 2), (1, 2), (0, 3), (1, 3)])
+        freed = arena.tile([P, 2 * CHUNK], I32, name="freed", offset=4 * KEY_ROW_BYTES, align_bytes=64)
+        woven = weave_keys(0, 2, freed[:])
+        upper_woven = weave_keys(1, 2, woven_rows("wq_first"))
         score_pair(0, 0, "scalar")
         quantize_woven(0, 2, woven)
         score_pair(1, 0, "scalar")
-        upper_woven = weave_keys(1, 2, woven_rows())
-        woven = weave_keys(0, 3, ring.tile([P, 2 * CHUNK], I32, name="woven", tag="key_rows6", align_bytes=64)[:])
         quantize_woven(1, 2, upper_woven)
+        woven = weave_keys(0, 3, ring.tile([P, 2 * CHUNK], I32, name="woven", tag="key_rows6", align_bytes=64)[:])
         quantize_woven(0, 3, woven)
         score_pair(2, 0, "scalar")
         score_pair(3, 0, "vector")

@@ -23,6 +23,8 @@ PASS = 512
 CHUNK = 512
 HALF = 256
 BANKS = 8
+QUERY_TURN = 48
+LATE_ORDER = (0, 4, 5, 6, 1, 2, 3, 7)
 BANK_BYTES = 2048
 CAST_BUFS = 4
 KEY_ROW_BYTES = 8 * CHUNK
@@ -41,7 +43,8 @@ def tile_list_kvt_act_kernel(
         banks_taken = []
 
         def new_bank(width):
-            banks_taken.append(len(banks_taken) % BANKS)
+            turn = len(banks_taken) - QUERY_TURN
+            banks_taken.append(LATE_ORDER[turn % BANKS] if turn >= 0 else len(banks_taken) % BANKS)
             return psum.tile([P, width], F32, name="bank%d" % len(banks_taken), offset=BANK_BYTES * banks_taken[-1])
 
         def new_bank_pair():
@@ -422,25 +425,26 @@ def tile_list_kvt_act_kernel(
         keys(1, 0)
         keys(1, 1)
         wide_keys(1, 2, "scalar")
-        query_banks = {(b, mt): queries(b, mt) for b in range(2) for mt in range(4)}
-        quantize_keys(1, 0)
+        query_banks = {(0, mt): queries(0, mt) for mt in range(4)}
+        query_banks[1, 0] = queries(1, 0)
         empty_queries(0, 0, "vector")
-        empty_queries(1, 0, "scalar")
-        quantize_keys(1, 1)
-        quantize_queries(0)
-        query_rows[3] = late.tile([P, 8 * P], BF16, name="query_rows3", tag="wq1", align_bytes=256)
+        quantize_keys(1, 0)
         empty_queries(0, 1, "vector")
-        empty_queries(1, 1, "scalar")
-        for b in range(2):
-            empty_queries(b, 2, "scalar")
-        empty_queries(0, 3, "vector")
+        empty_queries(0, 2, "scalar")
+        empty_queries(1, 0, "scalar")
+        for mt in range(1, 4):
+            query_banks[1, mt] = queries(1, mt)
+        quantize_queries(0)
+        quantize_keys(1, 1)
+        query_rows[3] = late.tile([P, 8 * P], BF16, name="query_rows3", tag="wq1", align_bytes=256)
+        for mt in range(1, 4):
+            empty_queries(1, mt, "scalar")
         quantize_queries(1)
-        empty_queries(1, 3, "vector")
+        empty_queries(0, 3, "vector")
         quantize_queries(2)
         quantize_queries(3)
-        key_scales("ka_late_scales", "wq1", [(0, 2), (1, 2), (0, 3), (1, 3)])
-        freed = arena.tile([P, 2 * CHUNK], I32, name="freed", offset=4 * KEY_ROW_BYTES, align_bytes=64)
-        woven = weave_keys(0, 2, freed[:])
+        key_scales("ka_late_scales", "x0", [(0, 2), (1, 2), (0, 3), (1, 3)])
+        woven = weave_keys(0, 2, woven_rows("wq1"))
         upper_woven = weave_keys(1, 2, woven_rows("wq_first"))
         score_pair(0, 0, "scalar")
         quantize_woven(0, 2, woven)
@@ -450,8 +454,6 @@ def tile_list_kvt_act_kernel(
         quantize_woven(0, 3, woven)
         score_pair(2, 0, "scalar")
         score_pair(3, 0, "vector")
-        scores(0, 2 * CHUNK, CHUNK, "scalar")
-        store_scores(0, 2 * CHUNK, CHUNK)
         for s in range(4):
             rows = key_rows[1, 3][:, 4 * P * s : 4 * P * (s + 1)]
             bank = features(wk_c, wk_s, 1, lambda a: tab_operand(a, 3, P * s, P))
@@ -459,7 +461,7 @@ def tile_list_kvt_act_kernel(
             if s % 2 == 1:
                 first = HALF * (s // 2)
                 quantize(ka_c[1][:, 3 * CHUNK :], ka_s[1, 3], first, HALF, key_rows[1, 3][:, 4 * first : 4 * (first + HALF)])
-        last_tiles = [(mt, 2) for mt in range(1, 4)] + [(mt, 3) for mt in range(4)]
+        last_tiles = [(mt, c) for c in (2, 3) for mt in range(4)]
         for n, (mt, c) in enumerate(last_tiles):
             for h in range(2):
                 scores(mt, CHUNK * c + HALF * h, HALF, "vector" if h == 1 and n > 0 else "scalar")

from contextlib import ExitStack

import concourse.mybir as mybir

K, R, M, N, T, J = 1024, 1024, 512, 512, 4096, 2048
FLOPS = 2 * (K * R * M + K * R * J + R * M * J + K * N * J)

F32 = mybir.dt.float32
BF16 = mybir.dt.bfloat16
I32 = mybir.dt.int32
U32 = mybir.dt.uint32
U16 = mybir.dt.uint16
U8 = mybir.dt.uint8
FP8X4 = mybir.dt.float8_e4m3fn_x4
FP4X4 = mybir.dt.float4_e2m1fn_x4
RELU = mybir.ActivationFunctionType.Relu
COPY = mybir.ActivationFunctionType.Copy
MAX = mybir.AluOpType.max
MULT = mybir.AluOpType.mult

P = 128
PASS = 512
CHUNK = 512
HALF = 256
BANKS = 8
QUERY_TURN = 48
LATE_ORDER = (0, 4, 5, 6, 1, 2, 3, 7)
BANK_BYTES = 2048
CAST_BUFS = 4
KEY_ROW_BYTES = 8 * CHUNK
ARENA_KEY_ROWS = 6
SCORE_SCALE = 0.03125


def tile_list_kvt_act_kernel(
    tc, tab_words, tab_scales, x, wq, wk, wv, offs, out_0, out_1
):
    nc = tc.nc
    with ExitStack() as ctx:
        keep = ctx.enter_context(tc.tile_pool(name="keep", bufs=1))
        ring = ctx.enter_context(tc.tile_pool(name="ring", bufs=1))
        psum = ctx.enter_context(tc.psum_pool(name="psum", bufs=1))
        banks_taken = []

        def new_bank(width):
            turn = len(banks_taken) - QUERY_TURN
            banks_taken.append(LATE_ORDER[turn % BANKS] if turn >= 0 else len(banks_taken) % BANKS)
            return psum.tile([P, width], F32, name="bank%d" % len(banks_taken), offset=BANK_BYTES * banks_taken[-1])

        def new_bank_pair():
            banks_taken.extend([len(banks_taken) % BANKS, len(banks_taken) % BANKS + 1])
            pair = psum.tile([P, 2 * CHUNK], F32, name="pair%d" % len(banks_taken), offset=BANK_BYTES * banks_taken[-2])
            return [pair[:, CHUNK * s : CHUNK * (s + 1)] for s in range(2)]

        offsets = keep.tile([P, J // 16], U16, name="offsets")
        arena = ctx.enter_context(tc.tile_pool(name="arena", bufs=1))
        table_words = arena.tile([P, T], I32, name="table_words", offset=0, align_bytes=64)
        operands = ctx.enter_context(tc.tile_pool(name="operands", bufs=1))
        ends = [0]

        def operand(name, dtype, width, size, start):
            offset = (ends[-1] - start + 255) // 256 * 256 + start
            ends.append(offset + width * size)
            return operands.tile([P, width], dtype, name=name, offset=offset, align_bytes=64 if start else 256)

        tab_codes = {}

        def codes_pair(name, width, code_start, scale_start):
            return (
                [operand("%s_codes%d" % (name, a), U32, width, 4, code_start) for a in range(2)],
                [operand("%s_scales%d" % (name, a), U8, width, 1, scale_start) for a in range(2)],
            )

        wv_ops = {}
        wk_c, wk_s = codes_pair("wk", R, 0, 64)
        wq_c, wq_s = codes_pair("wq", R, 0, 64)
        x_c, x_s = codes_pair("x", M, 128, 192)
        qa_c = operand("qa_codes", U32, 2 * M, 4, 0)
        qa_s = operand("qa_scales", U8, 2 * M, 1, 64)
        ka_c = [operand("ka_codes%d" % b, U32, J, 4, 128) for b in range(2)]
        picked_scales = operand("picked_scales", U8, J, 1, 192)
        second_scales = operand("second_scales", I32, J // 4, 4, 192)

        def load(raw, w, a, c0, width):
            nc.sync.dma_start(raw, w[PASS * a : PASS * (a + 1), c0 : c0 + width].rearrange("(p j) c -> p j c", j=4))
            return raw

        def staging(dtype, width, tag):
            bufs = CAST_BUFS if tag == "cast" else 1
            return ring.tile([P, width], dtype, name="staging", tag=tag, bufs=bufs, align_bytes=256)

        def round_plain(engine, raw, width, tag):
            grouped = staging(BF16, 4 * width, tag)
            out = grouped[:].rearrange("p (c i j) -> p c j i", i=4, j=4)
            in_ = raw.rearrange("p j (c i) -> p c j i", i=4)
            if engine == "scalar":
                nc.scalar.copy(out, in_)
            else:
                nc.vector.tensor_copy(out, in_)
            return grouped

        def round_permuted(engine, raw, h, tag):
            grouped = staging(BF16, 4 * HALF, tag)
            out = grouped[:].rearrange("p (t c i j) -> p t c j i", t=2, i=4, j=4)
            in_ = raw.rearrange("p j (c t i) -> p t c j i", t=4, i=4)[:, 2 * h : 2 * h + 2]
            if engine == "scalar":
                nc.scalar.copy(out, in_)
            else:
                nc.vector.tensor_copy(out, in_)
            return grouped

        def quantize(codes, scales, c0, width, grouped):
            nc.vector.quantize_mx(
                out=codes[:, c0 : c0 + width].bitcast(FP8X4), scales=scales[:, c0 : c0 + width], in_=grouped
            )

        def gather_words(c, picked):
            nc.vector.tensor_copy(picked[:], table_words[:].bitcast(U32).indirect(offsets[:, 32 * c : 32 * (c + 1)]))
            return picked

        def part_words(c, picked, tag, passes=(0, 1)):
            count = len(passes)
            padded = ring.tile([P, count * CHUNK + 64], U16, name="tab_codes", tag=tag, bufs=1, align_bytes=256)
            words = picked[:].bitcast(U16).rearrange("p (j d) -> p d j", d=2)[:, passes[0] : passes[0] + count]
            nc.vector.tensor_copy(padded[:, 64:].rearrange("p (d j) -> p d j", d=count), words)
            for n, a in enumerate(passes):
                tab_codes[a, c] = padded[:, 64 + CHUNK * n : 64 + CHUNK * (n + 1)]

        def tab_operand(a, c, j0, width):
            codes = tab_codes[a, c][:, j0 : j0 + width].bitcast(U8).bitcast(FP4X4)
            scale_rows = picked_scales[:] if a == 0 else second_scales[:].bitcast(U8)
            return codes, scale_rows[:, CHUNK * c + j0 : CHUNK * c + j0 + width]

        def two_passes(out, lhs_c, lhs_s, m0, rhs_of_pass, order=(0, 1)):
            for a in order:
                codes, scales = rhs_of_pass(a)
                nc.tensor.matmul_mx(
                    out=out,
                    lhsT=lhs_c[a][:, m0 : m0 + P].bitcast(FP8X4),
                    lhsT_scale=lhs_s[a][:, m0 : m0 + P],
                    rhs=codes,
                    rhs_scale=scales,
                    start=(a == order[0]),
                    stop=(a == order[1]),
                )

        def empty_features(bank, engine, rows):
            view_out = rows.rearrange("p (j t) -> p j t", t=4)
            view_in = bank.rearrange("p (t j) -> p j t", t=4)
            if engine == "scalar":
                nc.scalar.activation(view_out, view_in, RELU)
            else:
                nc.vector.tensor_scalar(view_out, view_in, 0.0, None, MAX)

        def features(w_c, w_s, b, rhs_of_pass):
            bank = new_bank(CHUNK)
            for t in range(4):
                two_passes(bank[:, P * t : P * (t + 1)], w_c, w_s, PASS * b + P * t, rhs_of_pass)
            return bank[:]

        def feature_pair(w_c, w_s, b, rhs_of_bank):
            banks = new_bank_pair()
            for t in range(4):
                cols = slice(PASS * b + P * t, PASS * b + P * (t + 1))
                for a in range(2):
                    for s in range(2):
                        codes, scales = rhs_of_bank(s, a)
                        nc.tensor.matmul_mx(
                            out=banks[s][:, P * t : P * (t + 1)],
                            lhsT=w_c[a][:, cols].bitcast(FP8X4),
                            lhsT_scale=w_s[a][:, cols],
                            rhs=codes,
                            rhs_scale=scales,
                            start=(a == 0),
                            stop=(a == 1),
                        )
            return banks

        def first_keys(count):
            pairs = [new_bank_pair() for u in range(count)]
            for a in range(2):
                for u in range(count):
                    for t in range(4):
                        for s in range(2):
                            codes, scales = tab_operand(a, 0, P * (2 * u + s), P)
                            nc.tensor.matmul_mx(
                                out=pairs[u][s][:, P * t : P * (t + 1)],
                                lhsT=wk_c[a][:, P * t : P * (t + 1)].bitcast(FP8X4),
                                lhsT_scale=wk_s[a][:, P * t : P * (t + 1)],
                                rhs=codes,
                                rhs_scale=scales,
                                start=(a == 0 and t == 0),
                                stop=(a == 1 and t == 3),
                            )
                    if a == 1:
                        for s in range(2):
                            n = 2 * u + s
                            empty_features(pairs[u][s], "scalar", key_rows[0, 0][:, 4 * P * n : 4 * P * (n + 1)])

        def values(groups, order):
            banks = [new_bank(CHUNK) for group in groups]
            for a in order:
                for bank, (nt, c) in zip(banks, groups):
                    codes, scales = tab_operand(a, c, 0, CHUNK)
                    nc.tensor.matmul_mx(
                        out=bank[:],
                        lhsT=wv_ops[a, nt][0].bitcast(FP8X4),
                        lhsT_scale=wv_ops[a, nt][1],
                        rhs=codes,
                        rhs_scale=scales,
                        start=(a == order[0]),
                        stop=(a == order[1]),
                    )
                    if a == order[1]:
                        nc.scalar.copy(value_rows[nt][:, CHUNK * c : CHUNK * (c + 1)], bank[:])

        def keys(b, c):
            for u in range(2):
                banks = feature_pair(wk_c, wk_s, b, lambda s, a: tab_operand(a, c, P * (2 * u + s), P))
                for s in range(2):
                    empty_features(banks[s], "scalar", key_rows[b, c][:, 4 * P * (2 * u + s) : 4 * P * (2 * u + s + 1)])

        def wide_keys(b, c, upper_engine):
            for u in range(2):
                for h in range(2):
                    bank = new_bank(CHUNK)
                    for t in range(2):
                        out = bank[:, HALF * t : HALF * (t + 1)]
                        two_passes(out, wk_c, wk_s, PASS * b + P * (2 * h + t), lambda a: tab_operand(a, c, HALF * u, HALF))
                    pairs = pair_rows[b, c, u][:, 2 * HALF * h : 2 * HALF * (h + 1)].rearrange("p (j t) -> p j t", t=2)
                    sums = bank[:].rearrange("p (t j) -> p j t", t=2)
                    if u == 0 or upper_engine == "scalar":
                        nc.scalar.activation(pairs, sums, RELU)
                    else:
                        nc.vector.tensor_scalar(pairs, sums, 0.0, None, MAX)

        def weave_keys(b, c, woven):
            if (b, c) == (0, 2):
                for u in range(2):
                    words = pair_rows[b, c, u].bitcast(I32).rearrange("p (h j) -> p j h", h=2)
                    nc.vector.tensor_copy(woven[:, CHUNK * u : CHUNK * (u + 1)].rearrange("p (j h) -> p j h", h=2), words)
            else:
                words = key_rows[b, c][:].bitcast(I32).rearrange("p (u h j) -> p u j h", u=2, h=2)
                nc.vector.tensor_copy(woven.rearrange("p (u j h) -> p u j h", u=2, h=2), words)
            return woven.bitcast(BF16)

        def woven_rows(tag):
            return late.tile([P, 2 * CHUNK], I32, name="woven", tag=tag, align_bytes=256)[:]

        def quantize_woven(b, c, woven):
            quantize(ka_c[b][:, CHUNK * c : CHUNK * (c + 1)], ka_s[b, c], 0, CHUNK, woven)

        def quantize_keys(b, c):
            quantize(ka_c[b][:, CHUNK * c : CHUNK * (c + 1)], ka_s[b, c], 0, CHUNK, key_rows[b, c][:])

        def queries(b, mt):
            cols = slice(P * mt, P * (mt + 1))
            return features(wq_c, wq_s, b, lambda a: (x_c[a][:, cols].bitcast(FP8X4), x_s[a][:, cols]))

        def empty_queries(b, mt, engine):
            empty_features(query_banks[b, mt], engine, query_rows[mt][:, 4 * P * b : 4 * P * (b + 1)])

        def quantize_queries(mt):
            quantize(qa_c, qa_s, 2 * P * mt, 2 * P, query_rows[mt][:])

        def scores(mt, j0, width, engine):
            cols = slice(j0, j0 + width)
            bank = new_bank(width)
            c, first = divmod(j0, CHUNK)
            lhs_c = [qa_c[:, P * b :] for b in range(2)]
            lhs_s = [qa_s[:, P * b :] for b in range(2)]
            two_passes(
                bank[:], lhs_c, lhs_s, 2 * P * mt, lambda b: (ka_c[b][:, cols].bitcast(FP8X4), ka_s[b, c][:, first : first + width])
            )
            if engine == "scalar":
                nc.scalar.activation(score_rows[mt][:, cols], bank[:], COPY, scale=SCORE_SCALE)
            else:
                nc.vector.tensor_scalar(score_rows[mt][:, cols], bank[:], SCORE_SCALE, None, MULT)

        def store_scores(mt, j0, width):
            nc.sync.dma_start(out_0[P * mt : P * (mt + 1), j0 : j0 + width], score_rows[mt][:, j0 : j0 + width])

        def score_pair(mt, pair, second):
            j0 = 2 * CHUNK * pair
            scores(mt, j0, CHUNK, "scalar")
            scores(mt, j0 + CHUNK, CHUNK, second)
            store_scores(mt, j0, 2 * CHUNK)

        def round_wv(a, c0, width):
            raw = wv_raw[a, c0 // HALF][:, :, c0 % HALF : c0 % HALF + width]
            return round_plain("scalar", raw, width, "wv%d_%d" % (a, c0))

        def quantize_wv(a, c0, width, grouped):
            codes = operand("wv_codes%d_%d" % (a, c0), U32, width, 4, 0)
            scales = operand("wv_scales%d_%d" % (a, c0), U8, width, 1, 64)
            quantize(codes, scales, 0, width, grouped[:])
            for n in range(width // P):
                wv_ops[a, c0 // P + n] = (codes[:, P * n : P * (n + 1)], scales[:, P * n : P * (n + 1)])

        def wv_piece(a, c0, width):
            quantize_wv(a, c0, width, round_wv(a, c0, width))

        def feature_weights(codes, scales, raw, a, b, tags=("cast", "cast")):
            halves = [round_permuted("vector", raw, h, tags[h]) for h in range(2)]
            for h in range(2):
                quantize(codes[a], scales[a], PASS * b + HALF * h, HALF, halves[h][:])

        with tc.tile_pool(name="early", bufs=1) as early:
            table_scales = early.tile([P, T // 4], I32, name="table_scales")
            nc.vector.memset(second_scales[:], 0)
            nc.sync.dma_start(offsets[:], offs)
            scale_rows_hbm = tab_scales.rearrange("a q t -> (a q) t").bitcast(I32)
            nc.sync.dma_start(table_scales[0:P:4, :], tab_scales.rearrange("a q t -> q a t").bitcast(I32))
            for i in range(1, 4):
                rows = scale_rows_hbm[i : i + 16, :].unsqueeze(1).broadcast_to([16, 2, T // 4])
                nc.sync.dma_start(table_scales[i:P:4, :], rows)
            nc.sync.dma_start(table_words[:], tab_words[0].rearrange("p t b -> p (t b)").bitcast(I32))
            wv_raw = {}
            for a in range(2):
                low = arena.tile([P, 4, HALF], F32, name="wv_low%d" % a, offset=4 * T + 16 * HALF * a, align_bytes=64)
                wv_raw[a, 0] = load(low[:], wv, a, 0, HALF)
            wv_raw[1, 1] = load(ring.tile([P, 4, HALF], F32, name="wv_high1", align_bytes=256)[:], wv, 1, HALF, HALF)
            nc.vector.tensor_copy(picked_scales[:], table_scales[:].bitcast(U8).indirect(offsets[:]))
            picked_rows = picked_scales[:].bitcast(I32)
            for q in range(4):
                nc.sync.dma_start(second_scales[32 * q : 32 * q + 4, :], picked_rows[32 * q + 4 : 32 * q + 32 : 8, :])

        late = ctx.enter_context(tc.tile_pool(name="late", bufs=1))
        wv_raw[0, 1] = load(late.tile([P, 4, HALF], F32, name="wv_high0", tag="high", align_bytes=64)[:], wv, 0, HALF, HALF)
        wk_raw = {}
        for b in range(2):
            for a in range(2):
                raw = late.tile([P, 4, PASS], F32, name="wk_raw", tag="wk%d" % (2 * b + a), align_bytes=64)
                wk_raw[a, b] = load(raw[:], wk, a, PASS * b, PASS)
        x_raw = [
            load(late.tile([P, 4, M], F32, name="x_raw", tag="x%d" % a, align_bytes=256)[:], x, a, 0, M) for a in range(2)
        ]
        wq_first = load(late.tile([P, 4, R], F32, name="wq_first", tag="wq_first", align_bytes=256)[:], wq, 0, 0, R)
        wq_second = [
            load(late.tile([P, 4, PASS], F32, name="wq_second", tag="wq%d" % b, align_bytes=256)[:], wq, 1, PASS * b, PASS)
            for b in range(2)
        ]

        picked = gather_words(0, staging(U32, CHUNK, "cast"))
        part_words(0, picked, "tab0", (0,))
        wv_piece(0, 0, P)
        picked_next = gather_words(1, staging(U32, CHUNK, "wv0_0"))
        wv_piece(0, P, P)
        part_words(0, picked, "wv0_128", (1,))
        picked = picked_next
        wv_piece(1, 0, P)
        wv_piece(1, P, P)
        upper = round_wv(1, HALF, HALF)
        part_words(1, picked, "wv1_128")
        quantize_wv(1, HALF, HALF, upper)
        picked = gather_words(2, staging(U32, CHUNK, "wv1_256"))
        wv_piece(0, HALF, HALF)
        part_words(2, picked, "wv0_256")
        part_words(3, gather_words(3, staging(U32, CHUNK, "wv1_256")), "tab3")

        first_rows = late.tile([P, 2, J], F32, name="first_rows", tag="high", align_bytes=64)
        value_rows = [first_rows[:, nt] for nt in range(2)]
        value_rows.extend(ring.tile([P, J], F32, name="value_rows%d" % nt)[:] for nt in (2, 3))
        values([(0, 0), (1, 0)], (0, 1))
        for nt in range(2):
            values([(nt, 1)], (1, 0))
        values([(2, 0), (3, 0), (2, 1), (3, 1)], (1, 0))
        for c in (2, 3):
            for nt in range(4):
                values([(nt, c)], (1, 0))

        feature_weights(wk_c, wk_s, wk_raw[0, 0], 0, 0)
        feature_weights(wk_c, wk_s, wk_raw[1, 0], 1, 0)
        for a in range(2):
            feature_weights(wk_c, wk_s, wk_raw[a, 1], a, 1)
        for a in range(2):
            tags = ("cast", ("cast", "wv1_256")[a])
            halves = [round_plain("vector", x_raw[a][:, :, HALF * h : HALF * (h + 1)], HALF, tags[h]) for h in range(2)]
            for h in range(2):
                quantize(x_c[a], x_s[a], HALF * h, HALF, halves[h][:])
        key_rows = {}
        for n in range(8):
            if n < ARENA_KEY_ROWS:
                rows = arena.tile([P, 4 * CHUNK], BF16, name="key_rows%d" % n, offset=KEY_ROW_BYTES * n, align_bytes=64)
            else:
                rows = ring.tile([P, 4 * CHUNK], BF16, name="key_rows", tag="key_rows%d" % n, align_bytes=64)
            key_rows[divmod(n, 4)] = rows
        pair_rows = {
            (b, c, u): key_rows[b, c][:, 2 * CHUNK * u : 2 * CHUNK * (u + 1)]
            for b, c in [(0, 2), (0, 3), (1, 2)]
            for u in range(2)
        }
        pair_rows[0, 2, 1] = late.tile([P, 2 * CHUNK], BF16, name="pair_rows", tag="x1", align_bytes=256)[:]
        ka_s = {}

        def key_scales(name, tag, chunks):
            rows = late.tile([P, len(chunks) * CHUNK + 192], U8, name=name, tag=tag, align_bytes=256)
            for n, chunk in enumerate(chunks):
                ka_s[chunk] = rows[:, 192 + CHUNK * n : 192 + CHUNK * (n + 1)]

        early_scales = staging(U8, 2 * CHUNK + 192, "wv1_256")
        for c in range(2):
            ka_s[0, c] = early_scales[:, 192 + CHUNK * c : 192 + CHUNK * (c + 1)]
        first_keys(2)
        keys(0, 1)
        wide_keys(0, 2, "vector")
        for c in range(2):
            quantize_keys(0, c)
        for b in range(2):
            feature_weights(wq_c, wq_s, wq_first[:, :, PASS * b : PASS * (b + 1)], 0, b)
        for b in range(2):
            feature_weights(wq_c, wq_s, wq_second[b], 1, b, (("cast", "wv0_0")[b], "cast"))
        for nt in range(4):
            nc.sync.dma_start(out_1[P * nt : P * (nt + 1), :], value_rows[nt])

        key_scales("ka_middle_scales", "wq0", [(1, 0), (1, 1)])
        score_rows = [late.tile([P, J], F32, name="score_rows", tag="wk%d" % mt, align_bytes=64) for mt in range(4)]
        query_rows = {
            0: late.tile([P, 8 * P], BF16, name="query_rows0", tag="wq1", align_bytes=256),
            1: staging(BF16, 8 * P, "wv0_0"),
            2: late.tile([P, 8 * P], BF16, name="query_rows2", tag="wq_first", align_bytes=256),
        }

        wide_keys(0, 3, "scalar")
        keys(1, 0)
        keys(1, 1)
        wide_keys(1, 2, "scalar")
        query_banks = {(0, mt): queries(0, mt) for mt in range(4)}
        query_banks[1, 0] = queries(1, 0)
        empty_queries(0, 0, "vector")
        quantize_keys(1, 0)
        empty_queries(0, 1, "vector")
        empty_queries(0, 2, "scalar")
        empty_queries(1, 0, "scalar")
        for mt in range(1, 4):
            query_banks[1, mt] = queries(1, mt)
        quantize_queries(0)
        quantize_keys(1, 1)
        query_rows[3] = late.tile([P, 8 * P], BF16, name="query_rows3", tag="wq1", align_bytes=256)
        for mt in range(1, 4):
            empty_queries(1, mt, "scalar")
        quantize_queries(1)
        empty_queries(0, 3, "vector")
        quantize_queries(2)
        quantize_queries(3)
        key_scales("ka_late_scales", "x0", [(0, 2), (1, 2), (0, 3), (1, 3)])
        woven = weave_keys(0, 2, woven_rows("wq1"))
        upper_woven = weave_keys(1, 2, woven_rows("wq_first"))
        score_pair(0, 0, "scalar")
        quantize_woven(0, 2, woven)
        score_pair(1, 0, "scalar")
        quantize_woven(1, 2, upper_woven)
        woven = weave_keys(0, 3, ring.tile([P, 2 * CHUNK], I32, name="woven", tag="key_rows6", align_bytes=64)[:])
        quantize_woven(0, 3, woven)
        score_pair(2, 0, "scalar")
        score_pair(3, 0, "vector")
        for s in range(4):
            rows = key_rows[1, 3][:, 4 * P * s : 4 * P * (s + 1)]
            bank = features(wk_c, wk_s, 1, lambda a: tab_operand(a, 3, P * s, P))
            empty_features(bank, ("scalar", "vector")[s % 2], rows)
            if s % 2 == 1:
                first = HALF * (s // 2)
                quantize(ka_c[1][:, 3 * CHUNK :], ka_s[1, 3], first, HALF, key_rows[1, 3][:, 4 * first : 4 * (first + HALF)])
        last_tiles = [(mt, c) for c in (2, 3) for mt in range(4)]
        for n, (mt, c) in enumerate(last_tiles):
            for h in range(2):
                scores(mt, CHUNK * c + HALF * h, HALF, "vector" if h == 1 and n > 0 else "scalar")
                if n == len(last_tiles) - 1:
                    store_scores(mt, CHUNK * c + HALF * h, HALF)
            if n < len(last_tiles) - 1:
                store_scores(mt, CHUNK * c, CHUNK)
